import numpy as np, ml_dtypes
CORES = [2,3,42,43,82,83,122,123]
N = 8
import mx_ref
BF = ml_dtypes.bfloat16
def entries(a):
    return np.ascontiguousarray(a.T).reshape(-1)
def table(e):
    return np.ascontiguousarray(np.reshape(e, (-1, 16)).T).astype(np.int32)
def cols(t, e):
    v = np.concatenate([t.reshape(128, -1, 4), np.zeros((128, 1, 4), BF)], axis=1)
    return np.ascontiguousarray(v[:, e]).reshape(128, -1)
def tile(rs):
    return np.stack(rs, axis=2).reshape(128, -1).astype(BF)
def cut(t, i, w=512):
    return t[:, w * i:w * i + w]
def f(rng, *shape):
    return mx_ref.flush((rng.standard_normal(shape, dtype=np.float32) * np.exp2(rng.integers(-2, 3, shape[:-1] + (1,)))).astype(BF))
def wide(rng, *shape, cols=0):
    v = rng.standard_normal(shape, dtype=np.float32) * np.exp2(rng.integers(-12, 13, shape)).astype(np.float32)
    if cols: v *= np.repeat(np.exp2(rng.integers(-cols, cols + 1, shape[:-2] + (1, shape[-1] // 4))) * (rng.random(shape[:-2] + (1, shape[-1] // 4)) > 0.0625), 4, axis=-1).astype(np.float32)
    return mx_ref.flush(v.astype(BF))
T, CAPA, CAPB, TR = 512, 96, 112, 16
def mix(rng, n, la=0, lb=0):
    n = n.copy()
    for _ in range(4000):
        p, q = rng.integers(0, N, (2, 3)); k = rng.integers(0, 4)
        p2, q2 = p.copy(), q.copy(); m = n.copy()
        if k == 3: p2[1] = q[1]
        else: p2[k], q2[k] = q[k], p[k]
        m[tuple(p)] -= 1; m[tuple(p2)] += 1
        if k < 3: m[tuple(q)] -= 1; m[tuple(q2)] += 1
        sa, ab = m.sum(axis=2), m.sum(axis=0)
        if m.min() >= 0 and m.max() <= TR and (sa <= CAPA).all() and (sa >= la).all() and (ab <= CAPB).all() and (ab >= lb).all(): n = m
    return n
def even():
    return np.full((N, N, N), T // N ** 2)
def places(rng, k, cap, by=None):
    out = np.zeros(len(k), int)
    for g in np.unique(k):
        j = np.flatnonzero(k == g)
        if by is None: out[j] = g * cap + rng.permutation(cap)[:len(j)]
        else: out[j[np.argsort(by[j])]] = g * cap + cap - 1 - np.arange(len(j))
    return out
def lists(rng, n, back=False):
    s, a, b = np.repeat(np.argwhere(n >= 0), n.reshape(-1), axis=0).T
    col = np.concatenate([rng.permutation(T) for r in range(N)])
    snd, pas, tri = np.full(N * N * CAPA, -1), np.full(N * N * CAPB, -1), np.full(N * N * N * TR, -1)
    p1 = places(rng, s * N + a, CAPA, col if back else None); snd[p1] = col
    arr = s * CAPA + p1 % CAPA
    p2 = places(rng, a * N + b, CAPB, arr if back else None); pas[p2] = arr
    p3 = places(rng, (s * N + a) * N + b, TR, col if back else None); tri[p3] = col
    c, t = a * CAPB + p2 % CAPB, (s * N + a) * TR + p3 % TR
    plc, plt = [], []
    for r in range(N):
        j = rng.permutation(np.flatnonzero(b == r))
        if back: j = j[np.argsort(-c[j])]
        plc.append(table(c[j])); plt.append(table(t[j]))
    return {"snd": np.stack([table(v) for v in snd.reshape(N, -1)]), "pas": np.stack([table(v) for v in pas.reshape(N, -1)]), "tri": np.stack([table(v) for v in tri.reshape(N, -1)]), "plc": np.stack(plc), "plt": np.stack(plt)}
def values(rng):
    return {"x": f(rng, N, 128, 4 * T), "w": f(rng, N, 128, 2048), "vv": f(rng, N, 128, 512)}
def setup_inputs(rng):
    return {**values(rng), **lists(rng, mix(rng, even()))}
def heavy(rng, d):
    n = even()
    for k in range(CAPB // N - T // N ** 2):
        for s in range(N):
            for a in range(N):
                n[s, a, (a + d) % N] += 1; n[s, a, (a + d + 1 + (s + k) % (N - 1)) % N] -= 1
    return {**values(rng), **lists(rng, mix(rng, n, lb=CAPB * np.roll(np.eye(N, dtype=int), d, axis=1)))}
def setup_inputs_diag(rng):
    return heavy(rng, 0)
def setup_inputs_onward(rng):
    return heavy(rng, int(rng.integers(1, N)))
def setup_inputs_full(rng):
    k = T // CAPA
    g = np.zeros((N, N), int); g[:, :k] = CAPA; g[:, k] = T - k * CAPA
    g = np.stack([np.roll(g[s], s) for s in range(N)])[rng.permutation(N)][:, rng.permutation(N)]
    return {**values(rng), **lists(rng, mix(rng, np.repeat(g[:, :, None] // N, N, axis=2), la=np.where(g == CAPA, CAPA, 0)))}
def setup_inputs_reversed(rng):
    return {**values(rng), **lists(rng, mix(rng, even()), back=True)}
def setup_inputs_spread(rng):
    d = setup_inputs(rng); d["x"] = wide(rng, N, 128, 4 * T); return d
def check_inputs(d):
    b = []
    snd, pas, tri, plc, plt = [[entries(d[k][r]) for r in range(N)] for k in ("snd", "pas", "tri", "plc", "plt")]
    for r in range(N):
        if snd[r].min() < -1 or not np.array_equal(np.sort(snd[r][snd[r] >= 0]), np.arange(T)): b.append("snd")
        if tri[r].min() < -1 or not np.array_equal(np.sort(tri[r][tri[r] >= 0]), np.arange(T)): b.append("tri")
        for a in range(N):
            u, v = snd[r][a * CAPA:(a + 1) * CAPA], tri[r][a * N * TR:(a + 1) * N * TR]
            if not np.array_equal(np.sort(u[u >= 0]), np.sort(v[v >= 0])): b.append("tri")
    arrived = [np.concatenate([snd[s][a * CAPA:(a + 1) * CAPA] for s in range(N)]) for a in range(N)]
    for a in range(N):
        if pas[a].min() < -1 or not np.array_equal(np.sort(pas[a][pas[a] >= 0]), np.flatnonzero(arrived[a] >= 0)): b.append("pas")
    if b: return b
    for r in range(N):
        k = np.concatenate([pas[a][r * CAPB:(r + 1) * CAPB] for a in range(N)])
        t = np.concatenate([tri[s][(a * N + r) * TR:(a * N + r + 1) * TR] for s in range(N) for a in range(N)])
        if not np.array_equal(np.sort(plc[r]), np.flatnonzero(k >= 0)): b.append("plc"); continue
        if not np.array_equal(np.sort(plt[r]), np.flatnonzero(t >= 0)): b.append("plt"); continue
        a, m = plc[r] // CAPB, k[plc[r]]
        if (plt[r] // TR != m // CAPA * N + a).any() or (t[plt[r]] != np.stack(arrived)[a, m]).any(): b.append("plt")
    return b
def reference(x, w, vv, snd, pas, tri, plc, plt):
    h = []
    for a in range(N):
        q = mx_ref.quantize(np.concatenate([cols(x[s], entries(snd[s])[a * CAPA:(a + 1) * CAPA]) for s in range(N)], axis=1))
        h.append(tile([np.maximum(mx_ref.matmul(mx_ref.quantize(cut(w[a], i)), q), np.float32(0)) * np.float32(0.043) for i in range(4)]))
    y = np.zeros((N, 128, T), np.float32)
    for b in range(N):
        t = np.concatenate([cols(h[a], entries(pas[a])[b * CAPB:(b + 1) * CAPB]) for a in range(N)], axis=1)
        y[b] = mx_ref.matmul(mx_ref.quantize(vv[b]), mx_ref.quantize(cols(t, entries(plc[b]))))
    return {"y": y}

@@ -1,0 +1,312 @@
+from concourse.bass import DstId, RemoteDMATransfer
+from concourse.mybir import AluOpType, ActivationFunctionType, dt
+
+N, TOK, TR = 8, 512, 16
+B = N * TR
+ALL = N * B
+HB = B // 2
+HA = ALL // 2
+
+SCRATCH = {
+    "trib": ("sbuf", [128, ALL // 16], "int32"),
+    "off1": ("sbuf", [128, ALL // 16], "uint16"),
+    "pltb": ("sbuf", [128, TOK // 16], "int32"),
+    "off2": ("sbuf", [128, TOK // 16], "uint16"),
+    "xb": ("sbuf", [128, 4 * TOK], "bfloat16"),
+    "wb": ("sbuf", [128, 2048], "bfloat16"),
+    "vb": ("sbuf", [128, 512], "bfloat16"),
+    "xg": ("sbuf", [128, 4 * ALL], "bfloat16"),
+    "wq": ("sbuf", [128, 512], "float8_e4m3fn_x4"),
+    "ws": ("sbuf", [128, 512], "uint8"),
+    "vq": ("sbuf", [128, 128], "float8_e4m3fn_x4"),
+    "vs": ("sbuf", [128, 128], "uint8"),
+    "xq": ("sbuf", [128, ALL], "float8_e4m3fn_x4"),
+    "xs": ("sbuf", [128, ALL], "uint8"),
+    "aq": ("sbuf", [128, ALL], "float8_e4m3fn_x4"),
+    "as_": ("sbuf", [128, ALL], "uint8"),
+    "rq": ("sbuf", [128, B], "float8_e4m3fn_x4"),
+    "rs": ("sbuf", [128, B], "uint8"),
+    "yv": ("sbuf", [128, ALL], "float32"),
+    "yt": ("sbuf", [128, TOK], "float32"),
+    "ps": ("psum", [128, 4096], "float32"),
+}
+for _f in range(2):
+    SCRATCH["h%d" % _f] = ("sbuf", [128, 4 * HA], "bfloat16")
+    SCRATCH["hq%d" % _f] = ("sbuf", [128, HA], "float8_e4m3fn_x4")
+    SCRATCH["hs%d" % _f] = ("sbuf", [128, HA], "uint8")
+    SCRATCH["bq%d" % _f] = ("sbuf", [128, 7 * HB], "float8_e4m3fn_x4")
+    SCRATCH["bs%d" % _f] = ("sbuf", [128, 7 * HB], "uint8")
+for _f in range(10):
+    SCRATCH["n%d" % _f] = ("sbuf", [128, TOK // 16], "int32")
+SEMAPHORES = (["ld_tri", "ld_x", "ld_w", "ld_v", "ld_plt", "off1r", "off2r", "wqr", "vqr", "pt",
+               "ls", "fc", "fcs", "yv0", "yv1", "st0", "st1", "viaq", "vias"]
+              + ["gx%d" % p for p in range(4)] + ["q1_%d" % p for p in range(4)]
+              + ["q2%d_%d" % (f, p) for p in range(4) for f in range(2)]
+              + ["in1_%d" % r for r in range(N)] + ["in2%d_%d" % (f, r) for r in range(N) for f in range(2)]
+              + ["ma%d" % k for k in range(N)] + ["mb%d" % k for k in range(N)] + ["rl%d" % k for k in range(N)]
+              + ["fm%d" % k for k in range(9)])
+
+
+def bits(engines):
+    return sum(1 << e for e in engines)
+
+
+def via(r, T, topo):
+    c = T.cores[r]
+    free = [o for o in topo.cores_of(c) if topo.die(o) != topo.die(c) and T.rank_of(o) is None
+            and all(topo.may_write(o, d) for d in T.cores if topo.chip(d) != topo.chip(c))]
+    return free[[d for d in T.cores if topo.chip(d) == topo.chip(c)].index(c)]
+
+
+def rank_program(g, core, T, topo):
+    rank = T.rank_of(core)
+    hands_on = rank is None
+    if hands_on:
+        served = [r for r in range(N) if via(r, T, topo) == core]
+        if not served:
+            return
+        rank = served[0]
+    S = T.sem
+    A = AluOpType
+    F = ActivationFunctionType
+    V, E, C = g.vector, g.tensor, g.scalar
+    chips = []
+    for c in T.cores:
+        if topo.chip(c) not in chips:
+            chips.append(topo.chip(c))
+    groups = [[r for r in range(N) if topo.chip(T.cores[r]) == c] for c in chips]
+    me = chips.index(topo.chip(core))
+    G = len(groups)
+    out_order = [(me + d) % G for d in range(1, G)]
+    in_order = [(me - d) % G for d in range(1, G)]
+    sib = [r for r in groups[me] if r != rank][0]
+    PC = 2 * B
+    far = topo.engines(core, T.cores[groups[out_order[0]][0]])
+    near = [e for e in topo.engines(core, T.cores[sib]) if e not in far][:len(far) // 2]
+    n = len(far) // 2
+
+    def share(ranks):
+        k = len(far) // len(ranks)
+        return [(r, far[k * i:k * (i + 1)]) for i, r in enumerate(ranks)]
+
+    def slot(b, a):
+        d = (b // 2 - a // 2) % G
+        return 6 if d == 0 else 2 * (d - 1) + a % 2
+
+    def views(src, dst, lo, to, w, code):
+        a, b = src[:, lo:lo + w], dst[:, to:to + w]
+        return (a.bitcast(dt.uint8), b.bitcast(dt.uint8)) if code else (a, b)
+
+    def send(dsts, src, dst, place, sem, code):
+        out = []
+        for r, eng in dsts:
+            rid, pid, _ = topo.addr(T.cores[r])
+            a, b = views(src, dst, *place(r), code)
+            out.append(RemoteDMATransfer(dst_ids=[DstId(rid=rid, pnc=pid)], dma_engine_mask=bits(eng),
+                                         remote_sem=S["%s_%d" % (sem, rank)], src=a, dst=b))
+        g.remote_dma_fused(out, local_sem=S["ls"])
+
+    last = out_order[G - 2]
+    if hands_on:
+        def place_on(r):
+            return HB * groups[last].index(r), HB * slot(r, rank), HB
+
+        g.wait_ge(S["viaq"], len(near))
+        send(share(groups[last]), T.rq, T.bq0, place_on, "in20", True)
+        g.wait_ge(S["vias"], len(near))
+        send(share(groups[last]), T.rs, T.bs0, place_on, "in20", False)
+        g.wait_ge(S["ls"], 2 * len(far))
+        return
+
+    for k in range(8):
+        q = g.sync if k < 3 else C
+        q.dma_start(T.trib[16 * k:16 * k + 16, :], T.tri[:]).then_inc(S["ld_tri"], 16)
+    g.sync.dma_start(T.xb[:], T.x[:]).then_inc(S["ld_x"], 16)
+    g.sync.wait_ge(S["ld_x"], 16)
+    g.sync.dma_start(T.wb[:], T.w[:]).then_inc(S["ld_w"], 16)
+    g.sync.dma_start(T.vb[:], T.vv[:]).then_inc(S["ld_v"], 16)
+    for k in range(8):
+        g.sync.dma_start(T.pltb[16 * k:16 * k + 16, :], T.plt[:]).then_inc(S["ld_plt"], 16)
+
+    V.wait_ge(S["ld_tri"], 128)
+    V.tensor_scalar(T.off1[:], T.trib[:], 4.0, 0.0, A.mult, A.max).then_inc(S["off1r"], 1)
+    V.wait_ge(S["off1r"], 1)
+    V.wait_ge(S["ld_x"], 16)
+    C.wait_ge(S["off1r"], 1)
+    C.wait_ge(S["ld_x"], 16)
+
+    def place1(r):
+        return B * r, B * rank, B
+
+    for p, gi in enumerate([out_order[0], me, out_order[1], out_order[2]]):
+        c0 = PC * gi
+        off = T.off1[:, c0 // 16:(c0 + PC) // 16]
+        ns = 3 if gi == me else 2
+        for t in range(4):
+            o = T.xg[:, 4 * c0 + t:4 * (c0 + PC):4]
+            i = T.xb[:, t:4 * TOK].indirect(off)
+            if t < ns:
+                C.activation(o, i, F.Copy).then_inc(S["gx%d" % p], 1)
+            else:
+                V.tensor_copy(o, i).then_inc(S["gx%d" % p], 1)
+        V.wait_ge(S["gx%d" % p], 4)
+        V.quantize_mx(T.xq[:, c0:c0 + PC], T.xs[:, c0:c0 + PC], T.xg[:, 4 * c0:4 * (c0 + PC)]).then_inc(S["q1_%d" % p], 1)
+        if gi == me:
+            continue
+        if p == 2:
+            g.wait_ge(S["q1_1"], 1)
+        g.wait_ge(S["q1_%d" % p], 1)
+        dst = share(groups[gi]) + ([(sib, near)] if p == 2 else [])
+        send(dst, T.xq, T.aq, place1, "in1", True)
+        send(dst, T.xs, T.as_, place1, "in1", False)
+
+    V.wait_ge(S["ld_w"], 16)
+    V.quantize_mx(T.wq[:], T.ws[:], T.wb[:]).then_inc(S["wqr"], 1)
+    V.wait_ge(S["ld_v"], 16)
+    V.quantize_mx(T.vq[:], T.vs[:], T.vb[:]).then_inc(S["vqr"], 1)
+
+    E.wait_ge(S["wqr"], 1)
+    halves = [[rank] + groups[in_order[0]] + [sib], groups[in_order[1]] + groups[in_order[2]]]
+    k = 0
+    for f, half in enumerate(halves):
+        h, hq, hs = T["h%d" % f], T["hq%d" % f], T["hs%d" % f]
+        for s in half:
+            if s == rank:
+                E.wait_ge(S["q1_1"], 1)
+                q, sc = T.xq, T.xs
+            else:
+                E.wait_ge(S["in1_%d" % s], 2 * n)
+                q, sc = T.aq, T.as_
+            if k >= 2:
+                E.wait_ge(S["rl%d" % (k - 2)], 4)
+            base = 2048 * (k % 2)
+            for i in (0, 2, 1, 3):
+                sem = S[("ma%d" if i < 2 else "mb%d") % k]
+                E.matmul_mx(T.ps[:, base + 512 * i:base + 512 * i + B], T.wq[:, 128 * i:128 * i + 128],
+                            T.ws[:, 128 * i:128 * i + 128], q[:, B * s:B * s + B], sc[:, B * s:B * s + B],
+                            True, True).then_inc(sem, 1)
+            C.wait_ge(S["ma%d" % k], 2)
+            V.wait_ge(S["mb%d" % k], 2)
+            place = 2 * ((me - s // 2) % G % 2) + s % 2
+            for i in range(4):
+                o = h[:, 4 * place + i:4 * HA:16]
+                z = T.ps[:, base + 512 * i:base + 512 * i + B]
+                if i < 2:
+                    C.activation(o, z, F.Relu, scale=0.043).then_inc(S["rl%d" % k], 1)
+                else:
+                    V.tensor_scalar(o, z, 0.0, 0.043, A.max, A.mult).then_inc(S["rl%d" % k], 1)
+            k += 1
+        for j in range(k - 4, k):
+            V.wait_ge(S["rl%d" % j], 4)
+        by = out_order + [me]
+        for p in ((2, 0, 1, 3) if f == 0 else (0, 1, 2, 3)):
+            c0 = B * by[p]
+            V.quantize_mx(hq[:, c0:c0 + B], hs[:, c0:c0 + B], h[:, 4 * c0:4 * (c0 + B)]).then_inc(S["q2%d_%d" % (f, p)], 1)
+
+        def place2(r):
+            return HB * r, HB * slot(r, rank), HB
+
+        if f == 0:
+            g.wait_ge(S["q20_2"], 1)
+            rid, pid, _ = topo.addr(via(rank, T, topo))
+            for src, dst, code, sem in ((hq, T.rq, True, "viaq"), (hs, T.rs, False, "vias")):
+                a, b = views(src, dst, B * last, 0, B, code)
+                g.remote_dma_fused([RemoteDMATransfer(dst_ids=[DstId(rid=rid, pnc=pid)], dma_engine_mask=bits(near),
+                                                      remote_sem=S[sem], src=a, dst=b)], local_sem=S["ls"])
+            calls = ((0, 1, 3),)
+        else:
+            calls = ((0, 1), (2, 3))
+        for ps in calls:
+            for p in ps:
+                g.wait_ge(S["q2%d_%d" % (f, p)], 1)
+            dst = share([r for p in ps if p < G - 1 for r in groups[by[p]]]) + ([(sib, near)] if 3 in ps else [])
+            send(dst, hq, T["bq%d" % f], place2, "in2%d" % f, True)
+            send(dst, hs, T["bs%d" % f], place2, "in2%d" % f, False)
+
+    cnt = [0]
+
+    def num(call, *args):
+        call(*args).then_inc(S["pt"], 1)
+        cnt[0] += 1
+
+    def done():
+        V.wait_ge(S["pt"], cnt[0])
+
+    t = [T["n%d" % i][:] for i in range(10)]
+    V.wait_ge(S["ld_plt"], 128)
+    num(V.tensor_scalar, t[0], T.pltb[:], 127, None, A.bitwise_and)
+    num(V.tensor_scalar, t[1], T.pltb[:], 5, 3, A.logical_shift_right, A.bitwise_and)
+    num(V.tensor_scalar, t[2], T.pltb[:], 8, None, A.logical_shift_right)
+    num(V.tensor_scalar, t[3], T.pltb[:], 7, 1, A.logical_shift_right, A.bitwise_and)
+    done()
+    num(V.tensor_tensor, t[4], t[1], t[2], A.subtract)
+    num(V.tensor_scalar, t[5], t[0], 4.0, None, A.mult)
+    done()
+    num(V.tensor_scalar, t[6], t[4], 1, 1, A.arith_shift_right, A.bitwise_and)
+    num(V.tensor_scalar, t[7], t[4], 1, None, A.bitwise_and)
+    num(V.tensor_tensor, t[8], t[5], t[3], A.add)
+    done()
+    num(V.tensor_scalar, t[1], t[6], 512.0, None, A.mult)
+    num(V.tensor_scalar, t[2], t[7], 2.0, None, A.mult)
+    done()
+    num(V.tensor_tensor, t[9], t[1], t[2], A.add)
+    done()
+    num(V.tensor_tensor, t[0], t[9], t[8], A.add)
+    done()
+    V.tensor_copy(T.off2[:], t[0]).then_inc(S["off2r"], 1)
+
+    E.wait_ge(S["vqr"], 1)
+    E.wait_ge(S["rl6"], 4)
+    E.wait_ge(S["rl7"], 4)
+    m = [0]
+
+    def product(bank, q, sc, lo, w, copies):
+        sem = S["fm%d" % m[0]]
+        m[0] += 1
+        E.matmul_mx(T.ps[:, 512 * bank:512 * bank + w], T.vq[:], T.vs[:], q[:, lo:lo + w], sc[:, lo:lo + w],
+                    True, True).then_inc(sem, 1)
+        for on, a, b, to, fin in copies:
+            z, y = T.ps[:, 512 * bank + a:512 * bank + a + b], T.yv[:, to:to + b]
+            if on == "V":
+                V.wait_ge(sem, 1)
+                V.tensor_copy(y, z).then_inc(S[fin], 1)
+            else:
+                C.wait_ge(sem, 1)
+                C.activation(y, z, F.Copy).then_inc(S[fin], 1)
+
+    for f in range(2):
+        hq, hs, bq, bs = T["hq%d" % f], T["hs%d" % f], T["bq%d" % f], T["bs%d" % f]
+        y0 = HA * f
+        E.wait_ge(S["q2%d_%d" % (f, G - 1)], 1)
+        if f:
+            E.wait_ge(S["fcs"], 1)
+        product(0, hq, hs, B * me, B, [("V", HB * (rank % 2), HB, y0 + HB * rank, "fc" if f else "fcs")])
+        for d in range(3):
+            for a in groups[in_order[d]]:
+                E.wait_ge(S["in2%d_%d" % (f, a)], n if d < 2 else 2 * n)
+            if d == 2:
+                E.wait_ge(S["in2%d_%d" % (f, sib)], 2 * len(near))
+            yd = y0 + B * in_order[d]
+            bank = 4 * f + d + (0 if f else 1)
+            on = "CVC"[d]
+            if d < 2:
+                product(bank, bq, bs, B * d, B, [(on, 0, B, yd, "fc")])
+            elif f == 0:
+                product(bank, bq, bs, B * d, B + HB, [(on, 0, B, yd, "fc"), (on, B, HB, y0 + HB * sib, "fc")])
+            else:
+                product(bank, bq, bs, B * d, B, [("C", 0, B, yd, "fc")])
+                product(bank + 1, bq, bs, B * d + HB, B, [("V", HB, HB, y0 + HB * sib, "fc")])
+    H = TOK // 2
+    for q in (C, V):
+        q.wait_ge(S["off2r"], 1)
+        q.wait_ge(S["fcs"], 1)
+        q.wait_ge(S["fc"], 9)
+    C.activation(T.yt[:, 0:H], T.yv[:].indirect(T.off2[:, 0:H // 16]), F.Copy).then_inc(S["yv0"], 1)
+    V.tensor_copy(T.yt[:, H:TOK], T.yv[:].indirect(T.off2[:, H // 16:TOK // 16])).then_inc(S["yv1"], 1)
+    C.wait_ge(S["yv0"], 1)
+    C.dma_start(T.y[:, 0:H], T.yt[:, 0:H]).then_inc(S["st0"], 16)
+    g.sync.wait_ge(S["yv1"], 1)
+    g.sync.dma_start(T.y[:, H:TOK], T.yt[:, H:TOK]).then_inc(S["st1"], 16)
+    C.wait_ge(S["st0"], 16)
+    g.sync.wait_ge(S["st1"], 16)
+    g.wait_ge(S["ls"], 12 * n + 2 * len(near) + (2 * len(far) + 4 * len(near)) + (4 * len(far) + 2 * len(near)))

@@ -6,6 +6,7 @@ B = N * TR
 ALL = N * B
 HB = B // 2
 HA = ALL // 2
+CODES, PLANE = "float8_e4m3fn_x4", "uint8"
 
 SCRATCH = {
     "trib": ("sbuf", [128, ALL // 16], "int32"),
@@ -16,42 +17,28 @@ SCRATCH = {
     "wb": ("sbuf", [128, 2048], "bfloat16"),
     "vb": ("sbuf", [128, 512], "bfloat16"),
     "xg": ("sbuf", [128, 4 * ALL], "bfloat16"),
-    "wq": ("sbuf", [128, 512], "float8_e4m3fn_x4"),
-    "ws": ("sbuf", [128, 512], "uint8"),
-    "vq": ("sbuf", [128, 128], "float8_e4m3fn_x4"),
-    "vs": ("sbuf", [128, 128], "uint8"),
-    "xq": ("sbuf", [128, ALL], "float8_e4m3fn_x4"),
-    "xs": ("sbuf", [128, ALL], "uint8"),
-    "aq": ("sbuf", [128, ALL], "float8_e4m3fn_x4"),
-    "as_": ("sbuf", [128, ALL], "uint8"),
-    "rq": ("sbuf", [128, B], "float8_e4m3fn_x4"),
-    "rs": ("sbuf", [128, B], "uint8"),
+    "h": ("sbuf", [128, 4 * HA], "bfloat16"),
     "yv": ("sbuf", [128, ALL], "float32"),
     "yt": ("sbuf", [128, TOK], "float32"),
     "ps": ("psum", [128, 4096], "float32"),
 }
-for _f in range(2):
-    SCRATCH["h%d" % _f] = ("sbuf", [128, 4 * HA], "bfloat16")
-    SCRATCH["hq%d" % _f] = ("sbuf", [128, HA], "float8_e4m3fn_x4")
-    SCRATCH["hs%d" % _f] = ("sbuf", [128, HA], "uint8")
-    SCRATCH["bq%d" % _f] = ("sbuf", [128, 7 * HB], "float8_e4m3fn_x4")
-    SCRATCH["bs%d" % _f] = ("sbuf", [128, 7 * HB], "uint8")
-for _f in range(10):
+for _name, _cols in (("w", 512), ("v", 128), ("x", ALL), ("h", HA), ("u", 512), ("r", 2 * B), ("a", HA),
+                     ("b", ALL - HB)):
+    SCRATCH[_name + "q"] = ("sbuf", [128, _cols], CODES)
+    SCRATCH[_name + "s_"] = ("sbuf", [128, _cols], PLANE)
+for _f in range(4):
     SCRATCH["n%d" % _f] = ("sbuf", [128, TOK // 16], "int32")
-SEMAPHORES = (["ld_tri", "ld_x", "ld_w", "ld_v", "ld_plt", "off1r", "off2r", "wqr", "vqr", "pt",
-               "ls", "fc", "fcs", "yv0", "yv1", "st0", "st1", "viaq", "vias"]
-              + ["gx%d" % p for p in range(4)] + ["q1_%d" % p for p in range(4)]
-              + ["q2%d_%d" % (f, p) for p in range(4) for f in range(2)]
-              + ["in1_%d" % r for r in range(N)] + ["in2%d_%d" % (f, r) for r in range(N) for f in range(2)]
-              + ["ma%d" % k for k in range(N)] + ["mb%d" % k for k in range(N)] + ["rl%d" % k for k in range(N)]
-              + ["fm%d" % k for k in range(9)])
+SEMAPHORES = (["ld_tri", "ld_x", "ld_w", "ld_w0", "wq0", "ld_v", "ld_plt", "off1r", "off2r", "wqr", "vqr", "pt",
+               "ls", "fc", "yv0", "yv1", "st0", "st1", "viaq", "vias", "inw"]
+              + [s + "%d" % p for p in range(4) for s in ("gx", "q1_", "q2_", "in1_", "ma", "mb", "rl")]
+              + ["in2_%d" % p for p in range(7)] + ["fm%d" % k for k in range(8)])
 
 
 def bits(engines):
     return sum(1 << e for e in engines)
 
 
-def via(r, T, topo):
+def helper(r, T, topo):
     c = T.cores[r]
     free = [o for o in topo.cores_of(c) if topo.die(o) != topo.die(c) and T.rank_of(o) is None
             and all(topo.may_write(o, d) for d in T.cores if topo.chip(d) != topo.chip(c))]
@@ -60,9 +47,9 @@ def via(r, T, topo):
 
 def rank_program(g, core, T, topo):
     rank = T.rank_of(core)
-    hands_on = rank is None
-    if hands_on:
-        served = [r for r in range(N) if via(r, T, topo) == core]
+    helps = rank is None
+    if helps:
+        served = [r for r in range(N) if helper(r, T, topo) == core]
         if not served:
             return
         rank = served[0]
@@ -77,230 +64,203 @@ def rank_program(g, core, T, topo):
     groups = [[r for r in range(N) if topo.chip(T.cores[r]) == c] for c in chips]
     me = chips.index(topo.chip(core))
     G = len(groups)
-    out_order = [(me + d) % G for d in range(1, G)]
-    in_order = [(me - d) % G for d in range(1, G)]
     sib = [r for r in groups[me] if r != rank][0]
     PC = 2 * B
-    far = topo.engines(core, T.cores[groups[out_order[0]][0]])
-    near = [e for e in topo.engines(core, T.cores[sib]) if e not in far][:len(far) // 2]
-    n = len(far) // 2
+    far = topo.engines(core, T.cores[groups[(me + 1) % G][0]])
+    near = [e for e in topo.engines(core, T.cores[sib]) if e not in far]
+    n = len(far)
 
-    def share(ranks):
-        k = len(far) // len(ranks)
-        return [(r, far[k * i:k * (i + 1)]) for i, r in enumerate(ranks)]
+    def ring(c):
+        return [(c + d) % G for d in range(1, G)]
 
-    def slot(b, a):
-        d = (b // 2 - a // 2) % G
-        return 6 if d == 0 else 2 * (d - 1) + a % 2
+    def order1(c):
+        return sorted(ring(c), key=lambda o: topo.same_plane(chips[c], chips[o]))
 
-    def views(src, dst, lo, to, w, code):
-        a, b = src[:, lo:lo + w], dst[:, to:to + w]
-        return (a.bitcast(dt.uint8), b.bitcast(dt.uint8)) if code else (a, b)
+    def worker(s, a):
+        return T.cores[a] if s % 2 == a % 2 else helper(a, T, topo)
 
-    def send(dsts, src, dst, place, sem, code):
-        out = []
-        for r, eng in dsts:
-            rid, pid, _ = topo.addr(T.cores[r])
-            a, b = views(src, dst, *place(r), code)
-            out.append(RemoteDMATransfer(dst_ids=[DstId(rid=rid, pnc=pid)], dma_engine_mask=bits(eng),
-                                         remote_sem=S["%s_%d" % (sem, rank)], src=a, dst=b))
-        g.remote_dma_fused(out, local_sem=S["ls"])
+    def share(items, engines):
+        k = len(engines) // len(items)
+        return [(it, engines[k * i:k * (i + 1)]) for i, it in enumerate(items)]
 
-    last = out_order[G - 2]
-    if hands_on:
-        def place_on(r):
-            return HB * groups[last].index(r), HB * slot(r, rank), HB
+    left = [0]
 
-        g.wait_ge(S["viaq"], len(near))
-        send(share(groups[last]), T.rq, T.bq0, place_on, "in20", True)
-        g.wait_ge(S["vias"], len(near))
-        send(share(groups[last]), T.rs, T.bs0, place_on, "in20", False)
-        g.wait_ge(S["ls"], 2 * len(far))
+    def move(to, engines, src, lo, dst, at, w, code, sem):
+        rid, pid, _ = topo.addr(to)
+        a, b = T[src + ("q" if code else "s_")][:, lo:lo + w], T[dst + ("q" if code else "s_")][:, at:at + w]
+        if code:
+            a, b = a.bitcast(dt.uint8), b.bitcast(dt.uint8)
+        left[0] += len(engines)
+        return RemoteDMATransfer(dst_ids=[DstId(rid=rid, pnc=pid)], dma_engine_mask=bits(engines),
+                                 remote_sem=S[sem], src=a, dst=b)
+
+    def send(moves):
+        g.remote_dma_fused(moves, local_sem=S["ls"])
+
+    def step1(ranks, engines, src, first, code):
+        return [move(worker(rank, a), eng, src, B * (a - first), "a", B * me, B, code, "in1_%d" % me)
+                for a, eng in share(ranks, engines)]
+
+    first, second, third = order1(me)
+    if helps:
+        g.wait_ge(S["viaq"], 2 * n)
+        send(step1(groups[first], far, "r", groups[first][0], True))
+        g.wait_ge(S["vias"], 2 * n)
+        send(step1(groups[first], far, "r", groups[first][0], False))
+        E.wait_ge(S["inw"], 4 * n)
+        wq, ws = T.uq, T.us_
+    else:
+        for k in range(2):
+            C.dma_start(T.trib[16 * k:16 * k + 16, :], T.tri[:]).then_inc(S["ld_tri"], 16)
+        g.sync.dma_start(T.wb[:, 0:512], T.w[:, 0:512]).then_inc(S["ld_w0"], 16)
+        g.sync.dma_start(T.xb[:], T.x[:]).then_inc(S["ld_x"], 16)
+        g.sync.dma_start(T.wb[:, 512:2048], T.w[:, 512:2048]).then_inc(S["ld_w"], 16)
+        g.sync.dma_start(T.vb[:], T.vv[:]).then_inc(S["ld_v"], 16)
+        for k in range(2):
+            g.sync.dma_start(T.pltb[16 * k:16 * k + 16, :], T.plt[:]).then_inc(S["ld_plt"], 16)
+
+        V.wait_ge(S["ld_tri"], 32)
+        for k in range(4):
+            V.tensor_scalar(T.off1[32 * k:32 * k + 32, :], T.trib[0:32, :], 4.0, 0.0, A.mult, A.max).then_inc(S["off1r"], 1)
+        mine = helper(rank, T, topo)
+        V.wait_ge(S["ld_w0"], 16)
+        V.quantize_mx(T.wq[:, 0:128], T.ws_[:, 0:128], T.wb[:, 0:512]).then_inc(S["wq0"], 1)
+        g.wait_ge(S["wq0"], 1)
+        send([move(mine, far + near, "w", 0, "u", 0, 128, True, "inw")])
+        for q in (V, C):
+            q.wait_ge(S["off1r"], 4)
+            q.wait_ge(S["ld_x"], 16)
+        for p, gi in enumerate([first, second, third, me]):
+            c0 = PC * gi
+            off = T.off1[:, c0 // 16:(c0 + PC) // 16]
+            for t in range(4):
+                o = T.xg[:, 4 * c0 + t:4 * (c0 + PC):4]
+                i = T.xb[:, t:4 * TOK].indirect(off)
+                if t < 2 + p % 2:
+                    C.activation(o, i, F.Copy).then_inc(S["gx%d" % p], 1)
+                else:
+                    V.tensor_copy(o, i).then_inc(S["gx%d" % p], 1)
+            if p == 1:
+                V.wait_ge(S["ld_w"], 16)
+                V.quantize_mx(T.wq[:, 128:512], T.ws_[:, 128:512], T.wb[:, 512:2048]).then_inc(S["wqr"], 1)
+                g.wait_ge(S["wqr"], 1)
+                send([move(mine, near, "w", 128, "u", 128, 384, True, "inw")])
+            V.wait_ge(S["gx%d" % p], 4)
+            V.quantize_mx(T.xq[:, c0:c0 + PC], T.xs_[:, c0:c0 + PC], T.xg[:, 4 * c0:4 * (c0 + PC)]).then_inc(S["q1_%d" % p], 1)
+            g.wait_ge(S["q1_%d" % p], 1)
+            if p == 0:
+                send([move(mine, far + near, "x", c0, "r", 0, PC, True, "viaq")])
+                send([move(mine, far + near, "x", c0, "r", 0, PC, False, "vias")])
+            elif p < 3:
+                send(step1(groups[gi], far, "x", 0, True)
+                     + ([move(mine, near, "w", 0, "u", 0, 512, False, "inw")] if p == 1 else []))
+                send(step1(groups[gi], far, "x", 0, False))
+            else:
+                send(step1([sib], near, "x", 0, True))
+                send(step1([sib], near, "x", 0, False))
+        E.wait_ge(S["wq0"], 1)
+        E.wait_ge(S["wqr"], 1)
+        wq, ws = T.wq, T.ws_
+
+    heard = {order1(c).index(me): c for c in ring(me)}
+    for m, k in enumerate([heard[1], me, heard[2], heard[0]]):
+        if k == me and not helps:
+            E.wait_ge(S["q1_3"], 1)
+            q, sc, lo = T.xq, T.xs_, B * rank
+        else:
+            E.wait_ge(S["in1_%d" % k], 2 * n if k == me else n)
+            q, sc, lo = T.aq, T.as_, B * k
+        if m >= 2:
+            E.wait_ge(S["rl%d" % (m - 2)], 4)
+        base = 2048 * (m % 2)
+        for i in (0, 2, 1, 3):
+            E.matmul_mx(T.ps[:, base + 512 * i:base + 512 * i + B], wq[:, 128 * i:128 * i + 128],
+                        ws[:, 128 * i:128 * i + 128], q[:, lo:lo + B], sc[:, lo:lo + B],
+                        True, True).then_inc(S[("ma%d" if i < 2 else "mb%d") % m], 1)
+        C.wait_ge(S["ma%d" % m], 2)
+        V.wait_ge(S["mb%d" % m], 2)
+        for i in range(4):
+            o = T.h[:, 4 * k + i:4 * HA:16]
+            z = T.ps[:, base + 512 * i:base + 512 * i + B]
+            if i < 2:
+                C.activation(o, z, F.Relu, scale=0.043).then_inc(S["rl%d" % m], 1)
+            else:
+                V.tensor_scalar(o, z, 0.0, 0.043, A.max, A.mult).then_inc(S["rl%d" % m], 1)
+    for m in range(4):
+        V.wait_ge(S["rl%d" % m], 4)
+    by = ring(me) + [me]
+    for p in range(G):
+        c0 = B * by[p]
+        V.quantize_mx(T.hq[:, c0:c0 + B], T.hs_[:, c0:c0 + B], T.h[:, 4 * c0:4 * (c0 + B)]).then_inc(S["q2_%d" % p], 1)
+
+    par = (rank + helps) % 2
+
+    def landing(b):
+        d = (b // 2 - me) % G
+        if d:
+            blk = 2 * (d - 1) + par
+            return blk, B * blk + HB * (rank % 2)
+        return 6, B * 6 + (HB * (rank % 2) if par != b % 2 else B)
+
+    def step2(ranks, engines, code):
+        return [move(T.cores[b], eng, "h", HB * b, "b", landing(b)[1], HB, code, "in2_%d" % landing(b)[0])
+                for b, eng in share(ranks, engines)]
+
+    here = groups[me] if helps else [sib]
+    for p in (0, 1):
+        g.wait_ge(S["q2_%d" % p], 1)
+    for code in (True, False):
+        send(step2(groups[by[0]] + groups[by[1]], far, code))
+    for p in (2, 3):
+        g.wait_ge(S["q2_%d" % p], 1)
+    for code in (True, False):
+        send(step2(groups[by[2]], far, code) + step2(here, near[:len(here) * n // 2], code))
+    if helps:
+        g.wait_ge(S["ls"], left[0])
         return
 
-    for k in range(8):
-        q = g.sync if k < 3 else C
-        q.dma_start(T.trib[16 * k:16 * k + 16, :], T.tri[:]).then_inc(S["ld_tri"], 16)
-    g.sync.dma_start(T.xb[:], T.x[:]).then_inc(S["ld_x"], 16)
-    g.sync.wait_ge(S["ld_x"], 16)
-    g.sync.dma_start(T.wb[:], T.w[:]).then_inc(S["ld_w"], 16)
-    g.sync.dma_start(T.vb[:], T.vv[:]).then_inc(S["ld_v"], 16)
-    for k in range(8):
-        g.sync.dma_start(T.pltb[16 * k:16 * k + 16, :], T.plt[:]).then_inc(S["ld_plt"], 16)
-
-    V.wait_ge(S["ld_tri"], 128)
-    V.tensor_scalar(T.off1[:], T.trib[:], 4.0, 0.0, A.mult, A.max).then_inc(S["off1r"], 1)
-    V.wait_ge(S["off1r"], 1)
-    V.wait_ge(S["ld_x"], 16)
-    C.wait_ge(S["off1r"], 1)
-    C.wait_ge(S["ld_x"], 16)
-
-    def place1(r):
-        return B * r, B * rank, B
-
-    for p, gi in enumerate([out_order[0], me, out_order[1], out_order[2]]):
-        c0 = PC * gi
-        off = T.off1[:, c0 // 16:(c0 + PC) // 16]
-        ns = 3 if gi == me else 2
-        for t in range(4):
-            o = T.xg[:, 4 * c0 + t:4 * (c0 + PC):4]
-            i = T.xb[:, t:4 * TOK].indirect(off)
-            if t < ns:
-                C.activation(o, i, F.Copy).then_inc(S["gx%d" % p], 1)
-            else:
-                V.tensor_copy(o, i).then_inc(S["gx%d" % p], 1)
-        V.wait_ge(S["gx%d" % p], 4)
-        V.quantize_mx(T.xq[:, c0:c0 + PC], T.xs[:, c0:c0 + PC], T.xg[:, 4 * c0:4 * (c0 + PC)]).then_inc(S["q1_%d" % p], 1)
-        if gi == me:
-            continue
-        if p == 2:
-            g.wait_ge(S["q1_1"], 1)
-        g.wait_ge(S["q1_%d" % p], 1)
-        dst = share(groups[gi]) + ([(sib, near)] if p == 2 else [])
-        send(dst, T.xq, T.aq, place1, "in1", True)
-        send(dst, T.xs, T.as_, place1, "in1", False)
-
-    V.wait_ge(S["ld_w"], 16)
-    V.quantize_mx(T.wq[:], T.ws[:], T.wb[:]).then_inc(S["wqr"], 1)
     V.wait_ge(S["ld_v"], 16)
-    V.quantize_mx(T.vq[:], T.vs[:], T.vb[:]).then_inc(S["vqr"], 1)
-
-    E.wait_ge(S["wqr"], 1)
-    halves = [[rank] + groups[in_order[0]] + [sib], groups[in_order[1]] + groups[in_order[2]]]
-    k = 0
-    for f, half in enumerate(halves):
-        h, hq, hs = T["h%d" % f], T["hq%d" % f], T["hs%d" % f]
-        for s in half:
-            if s == rank:
-                E.wait_ge(S["q1_1"], 1)
-                q, sc = T.xq, T.xs
-            else:
-                E.wait_ge(S["in1_%d" % s], 2 * n)
-                q, sc = T.aq, T.as_
-            if k >= 2:
-                E.wait_ge(S["rl%d" % (k - 2)], 4)
-            base = 2048 * (k % 2)
-            for i in (0, 2, 1, 3):
-                sem = S[("ma%d" if i < 2 else "mb%d") % k]
-                E.matmul_mx(T.ps[:, base + 512 * i:base + 512 * i + B], T.wq[:, 128 * i:128 * i + 128],
-                            T.ws[:, 128 * i:128 * i + 128], q[:, B * s:B * s + B], sc[:, B * s:B * s + B],
-                            True, True).then_inc(sem, 1)
-            C.wait_ge(S["ma%d" % k], 2)
-            V.wait_ge(S["mb%d" % k], 2)
-            place = 2 * ((me - s // 2) % G % 2) + s % 2
-            for i in range(4):
-                o = h[:, 4 * place + i:4 * HA:16]
-                z = T.ps[:, base + 512 * i:base + 512 * i + B]
-                if i < 2:
-                    C.activation(o, z, F.Relu, scale=0.043).then_inc(S["rl%d" % k], 1)
-                else:
-                    V.tensor_scalar(o, z, 0.0, 0.043, A.max, A.mult).then_inc(S["rl%d" % k], 1)
-            k += 1
-        for j in range(k - 4, k):
-            V.wait_ge(S["rl%d" % j], 4)
-        by = out_order + [me]
-        for p in ((2, 0, 1, 3) if f == 0 else (0, 1, 2, 3)):
-            c0 = B * by[p]
-            V.quantize_mx(hq[:, c0:c0 + B], hs[:, c0:c0 + B], h[:, 4 * c0:4 * (c0 + B)]).then_inc(S["q2%d_%d" % (f, p)], 1)
-
-        def place2(r):
-            return HB * r, HB * slot(r, rank), HB
-
-        if f == 0:
-            g.wait_ge(S["q20_2"], 1)
-            rid, pid, _ = topo.addr(via(rank, T, topo))
-            for src, dst, code, sem in ((hq, T.rq, True, "viaq"), (hs, T.rs, False, "vias")):
-                a, b = views(src, dst, B * last, 0, B, code)
-                g.remote_dma_fused([RemoteDMATransfer(dst_ids=[DstId(rid=rid, pnc=pid)], dma_engine_mask=bits(near),
-                                                      remote_sem=S[sem], src=a, dst=b)], local_sem=S["ls"])
-            calls = ((0, 1, 3),)
-        else:
-            calls = ((0, 1), (2, 3))
-        for ps in calls:
-            for p in ps:
-                g.wait_ge(S["q2%d_%d" % (f, p)], 1)
-            dst = share([r for p in ps if p < G - 1 for r in groups[by[p]]]) + ([(sib, near)] if 3 in ps else [])
-            send(dst, hq, T["bq%d" % f], place2, "in2%d" % f, True)
-            send(dst, hs, T["bs%d" % f], place2, "in2%d" % f, False)
-
-    cnt = [0]
-
-    def num(call, *args):
-        call(*args).then_inc(S["pt"], 1)
-        cnt[0] += 1
-
-    def done():
-        V.wait_ge(S["pt"], cnt[0])
-
-    t = [T["n%d" % i][:] for i in range(10)]
-    V.wait_ge(S["ld_plt"], 128)
-    num(V.tensor_scalar, t[0], T.pltb[:], 127, None, A.bitwise_and)
-    num(V.tensor_scalar, t[1], T.pltb[:], 5, 3, A.logical_shift_right, A.bitwise_and)
-    num(V.tensor_scalar, t[2], T.pltb[:], 8, None, A.logical_shift_right)
-    num(V.tensor_scalar, t[3], T.pltb[:], 7, 1, A.logical_shift_right, A.bitwise_and)
-    done()
-    num(V.tensor_tensor, t[4], t[1], t[2], A.subtract)
-    num(V.tensor_scalar, t[5], t[0], 4.0, None, A.mult)
-    done()
-    num(V.tensor_scalar, t[6], t[4], 1, 1, A.arith_shift_right, A.bitwise_and)
-    num(V.tensor_scalar, t[7], t[4], 1, None, A.bitwise_and)
-    num(V.tensor_tensor, t[8], t[5], t[3], A.add)
-    done()
-    num(V.tensor_scalar, t[1], t[6], 512.0, None, A.mult)
-    num(V.tensor_scalar, t[2], t[7], 2.0, None, A.mult)
-    done()
-    num(V.tensor_tensor, t[9], t[1], t[2], A.add)
-    done()
-    num(V.tensor_tensor, t[0], t[9], t[8], A.add)
-    done()
-    V.tensor_copy(T.off2[:], t[0]).then_inc(S["off2r"], 1)
+    V.quantize_mx(T.vq[:], T.vs_[:], T.vb[:]).then_inc(S["vqr"], 1)
+    t = [T["n%d" % i][0:32, :] for i in range(4)]
+    V.wait_ge(S["ld_plt"], 32)
+    V.tensor_scalar(t[0], T.pltb[0:32, :], 255, None, A.bitwise_and).then_inc(S["pt"], 1)
+    V.tensor_scalar(t[1], T.pltb[0:32, :], 8, None, A.logical_shift_right).then_inc(S["pt"], 1)
+    V.wait_ge(S["pt"], 2)
+    V.tensor_scalar(t[2], t[0], 4.0, None, A.mult).then_inc(S["pt"], 1)
+    V.wait_ge(S["pt"], 3)
+    V.tensor_tensor(t[3], t[2], t[1], A.add).then_inc(S["pt"], 1)
+    V.wait_ge(S["pt"], 4)
+    for k in range(4):
+        V.tensor_copy(T.off2[32 * k:32 * k + 32, :], t[3]).then_inc(S["off2r"], 1)
 
     E.wait_ge(S["vqr"], 1)
-    E.wait_ge(S["rl6"], 4)
-    E.wait_ge(S["rl7"], 4)
-    m = [0]
+    bank = [0]
+    copied = [0]
 
-    def product(bank, q, sc, lo, w, copies):
-        sem = S["fm%d" % m[0]]
-        m[0] += 1
-        E.matmul_mx(T.ps[:, 512 * bank:512 * bank + w], T.vq[:], T.vs[:], q[:, lo:lo + w], sc[:, lo:lo + w],
-                    True, True).then_inc(sem, 1)
-        for on, a, b, to, fin in copies:
-            z, y = T.ps[:, 512 * bank + a:512 * bank + a + b], T.yv[:, to:to + b]
-            if on == "V":
-                V.wait_ge(sem, 1)
-                V.tensor_copy(y, z).then_inc(S[fin], 1)
-            else:
-                C.wait_ge(sem, 1)
-                C.activation(y, z, F.Copy).then_inc(S[fin], 1)
+    def product(q, sc, lo, w, on, copies):
+        sem, b0 = S["fm%d" % bank[0]], 512 * bank[0]
+        bank[0] += 1
+        E.matmul_mx(T.ps[:, b0:b0 + w], T.vq[:], T.vs_[:], q[:, lo:lo + w], sc[:, lo:lo + w], True, True).then_inc(sem, 1)
+        on.wait_ge(sem, 1)
+        for a, b, to in copies:
+            z, y = T.ps[:, b0 + a:b0 + a + b], T.yv[:, to:to + b]
+            (V.tensor_copy(y, z) if on is V else C.activation(y, z, F.Copy)).then_inc(S["fc"], 1)
+            copied[0] += 1
 
-    for f in range(2):
-        hq, hs, bq, bs = T["hq%d" % f], T["hs%d" % f], T["bq%d" % f], T["bs%d" % f]
-        y0 = HA * f
-        E.wait_ge(S["q2%d_%d" % (f, G - 1)], 1)
-        if f:
-            E.wait_ge(S["fcs"], 1)
-        product(0, hq, hs, B * me, B, [("V", HB * (rank % 2), HB, y0 + HB * rank, "fc" if f else "fcs")])
-        for d in range(3):
-            for a in groups[in_order[d]]:
-                E.wait_ge(S["in2%d_%d" % (f, a)], n if d < 2 else 2 * n)
-            if d == 2:
-                E.wait_ge(S["in2%d_%d" % (f, sib)], 2 * len(near))
-            yd = y0 + B * in_order[d]
-            bank = 4 * f + d + (0 if f else 1)
-            on = "CVC"[d]
-            if d < 2:
-                product(bank, bq, bs, B * d, B, [(on, 0, B, yd, "fc")])
-            elif f == 0:
-                product(bank, bq, bs, B * d, B + HB, [(on, 0, B, yd, "fc"), (on, B, HB, y0 + HB * sib, "fc")])
-            else:
-                product(bank, bq, bs, B * d, B, [("C", 0, B, yd, "fc")])
-                product(bank + 1, bq, bs, B * d + HB, B, [("V", HB, HB, y0 + HB * sib, "fc")])
+    E.wait_ge(S["q2_3"], 1)
+    product(T.hq, T.hs_, B * me, B, C, [(HB * par, HB, HA * par + HB * rank)])
+    for d in range(1, G):
+        if d == G - 1:
+            E.wait_ge(S["in2_6"], 3 * n)
+            product(T.bq, T.bs_, 6 * B, B + HB, V, [(0, B, HA * (1 - par) + B * me), (B, HB, HA * par + HB * sib)])
+        for f in range(2):
+            blk = 2 * (d - 1) + f
+            E.wait_ge(S["in2_%d" % blk], n if d < G - 1 else 2 * n)
+            product(T.bq, T.bs_, B * blk, B, (C, V)[f], [(0, B, HA * f + B * ((me - d) % G))])
     H = TOK // 2
     for q in (C, V):
-        q.wait_ge(S["off2r"], 1)
-        q.wait_ge(S["fcs"], 1)
-        q.wait_ge(S["fc"], 9)
+        q.wait_ge(S["off2r"], 4)
+        q.wait_ge(S["fc"], copied[0])
     C.activation(T.yt[:, 0:H], T.yv[:].indirect(T.off2[:, 0:H // 16]), F.Copy).then_inc(S["yv0"], 1)
     V.tensor_copy(T.yt[:, H:TOK], T.yv[:].indirect(T.off2[:, H // 16:TOK // 16])).then_inc(S["yv1"], 1)
     C.wait_ge(S["yv0"], 1)
@@ -309,4 +269,4 @@ def rank_program(g, core, T, topo):
     g.sync.dma_start(T.y[:, H:TOK], T.yt[:, H:TOK]).then_inc(S["st1"], 16)
     C.wait_ge(S["st0"], 16)
     g.sync.wait_ge(S["st1"], 16)
-    g.wait_ge(S["ls"], 12 * n + 2 * len(near) + (2 * len(far) + 4 * len(near)) + (4 * len(far) + 2 * len(near)))
+    g.wait_ge(S["ls"], left[0])

@@ -6,6 +6,7 @@ B = N * TR
 ALL = N * B
 HB = B // 2
 HA = ALL // 2
+PC = 2 * B
 CODES, PLANE = "float8_e4m3fn_x4", "uint8"
 
 SCRATCH = {
@@ -22,15 +23,15 @@ SCRATCH = {
     "yt": ("sbuf", [128, TOK], "float32"),
     "ps": ("psum", [128, 4096], "float32"),
 }
-for _name, _cols in (("w", 512), ("v", 128), ("x", ALL), ("h", HA), ("u", 512), ("r", 2 * B), ("a", HA),
+for _name, _cols in (("w", 512), ("v", 128), ("x", ALL), ("h", HA), ("u", 512), ("r", PC), ("a", 12 * HB),
                      ("b", ALL - HB)):
     SCRATCH[_name + "q"] = ("sbuf", [128, _cols], CODES)
     SCRATCH[_name + "s_"] = ("sbuf", [128, _cols], PLANE)
 for _f in range(4):
     SCRATCH["n%d" % _f] = ("sbuf", [128, TOK // 16], "int32")
-SEMAPHORES = (["ld_tri", "ld_x", "ld_w", "ld_w0", "wq0", "ld_v", "ld_plt", "off1r", "off2r", "wqr", "vqr", "pt",
-               "ls", "fc", "yv0", "yv1", "st0", "st1", "viaq", "vias", "inw"]
-              + [s + "%d" % p for p in range(4) for s in ("gx", "q1_", "q2_", "in1_", "ma", "mb", "rl")]
+SEMAPHORES = (["ld_tri", "ld_x", "ld_w", "ld_w0", "wq0", "ld_v", "ld_plt", "off0r", "off1r", "off2r", "wqr", "vqr", "pt",
+               "ls", "fc", "ya0", "ya1", "yb0", "yb1", "st0", "st1", "viaq0", "viaq1", "vias0", "vias1", "inw"]
+              + [s + "%d" % p for p in range(5) for s in ("gx", "q1_", "q2_", "in1_", "rl", "m0_", "m1_", "m2_", "m3_")]
               + ["in2_%d" % p for p in range(7)] + ["fm%d" % k for k in range(8)])
 
 
@@ -65,16 +66,10 @@ def rank_program(g, core, T, topo):
     me = chips.index(topo.chip(core))
     G = len(groups)
     sib = [r for r in groups[me] if r != rank][0]
-    PC = 2 * B
-    far = topo.engines(core, T.cores[groups[(me + 1) % G][0]])
+    by = [(me + d) % G for d in range(1, G + 1)]
+    far = topo.engines(core, T.cores[groups[by[0]][0]])
     near = [e for e in topo.engines(core, T.cores[sib]) if e not in far]
     n = len(far)
-
-    def ring(c):
-        return [(c + d) % G for d in range(1, G)]
-
-    def order1(c):
-        return sorted(ring(c), key=lambda o: topo.same_plane(chips[c], chips[o]))
 
     def worker(s, a):
         return T.cores[a] if s % 2 == a % 2 else helper(a, T, topo)
@@ -97,124 +92,141 @@ def rank_program(g, core, T, topo):
     def send(moves):
         g.remote_dma_fused(moves, local_sem=S["ls"])
 
-    def step1(ranks, engines, src, first, code):
-        return [move(worker(rank, a), eng, src, B * (a - first), "a", B * me, B, code, "in1_%d" % me)
-                for a, eng in share(ranks, engines)]
+    def step1(f, items, engines, src, code):
+        out = []
+        for (a, lo), eng in share(items, engines):
+            d = (a // 2 - me) % G
+            place = d - 2 if d > 1 else 3 if d == 0 else 5 if a % 2 and rank % 2 else 2
+            out.append(move(worker(rank, a), eng, src, lo, "a", HB * (6 * f + place), HB, code, "in1_%d" % (2 * f + (d < 2))))
+        return out
 
-    first, second, third = order1(me)
     if helps:
-        g.wait_ge(S["viaq"], 2 * n)
-        send(step1(groups[first], far, "r", groups[first][0], True))
-        g.wait_ge(S["vias"], 2 * n)
-        send(step1(groups[first], far, "r", groups[first][0], False))
-        E.wait_ge(S["inw"], 4 * n)
+        for f in range(2):
+            for code in (True, False):
+                g.wait_ge(S[("viaq%d" if code else "vias%d") % f], n if f else 2 * n)
+                send(step1(f, [(a, B * f + HB * (a % 2)) for a in groups[by[0]]], far, "r", code))
+        E.wait_ge(S["inw"], 3 * n)
         wq, ws = T.uq, T.us_
     else:
+        g.sync.dma_start(T.wb[:, 0:512], T.w[:, 0:512]).then_inc(S["ld_w0"], 16)
         for k in range(2):
             C.dma_start(T.trib[16 * k:16 * k + 16, :], T.tri[:]).then_inc(S["ld_tri"], 16)
-        g.sync.dma_start(T.wb[:, 0:512], T.w[:, 0:512]).then_inc(S["ld_w0"], 16)
         g.sync.dma_start(T.xb[:], T.x[:]).then_inc(S["ld_x"], 16)
         g.sync.dma_start(T.wb[:, 512:2048], T.w[:, 512:2048]).then_inc(S["ld_w"], 16)
         g.sync.dma_start(T.vb[:], T.vv[:]).then_inc(S["ld_v"], 16)
         for k in range(2):
             g.sync.dma_start(T.pltb[16 * k:16 * k + 16, :], T.plt[:]).then_inc(S["ld_plt"], 16)
 
-        V.wait_ge(S["ld_tri"], 32)
-        for k in range(4):
-            V.tensor_scalar(T.off1[32 * k:32 * k + 32, :], T.trib[0:32, :], 4.0, 0.0, A.mult, A.max).then_inc(S["off1r"], 1)
         mine = helper(rank, T, topo)
         V.wait_ge(S["ld_w0"], 16)
         V.quantize_mx(T.wq[:, 0:128], T.ws_[:, 0:128], T.wb[:, 0:512]).then_inc(S["wq0"], 1)
         g.wait_ge(S["wq0"], 1)
         send([move(mine, far + near, "w", 0, "u", 0, 128, True, "inw")])
+
+        V.wait_ge(S["ld_tri"], 32)
+        made = 0
+        for f, c0 in enumerate((by[0], me)):
+            for lo, hi in ((c0, G), (0, c0)):
+                if hi > lo:
+                    to = 32 * f + 8 * ((lo - c0) % G)
+                    V.tensor_scalar(T.off1[0:32, to:to + 8 * (hi - lo)], T.trib[0:32, 16 * lo + f:16 * hi:2],
+                                    4.0, 0.0, A.mult, A.max).then_inc(S["off0r"], 1)
+                    made += 1
+        V.wait_ge(S["off0r"], made)
+        for k in range(1, 4):
+            V.tensor_copy(T.off1[32 * k:32 * k + 32, :], T.off1[0:32, :]).then_inc(S["off1r"], 1)
         for q in (V, C):
-            q.wait_ge(S["off1r"], 4)
+            q.wait_ge(S["off1r"], 3)
             q.wait_ge(S["ld_x"], 16)
-        for p, gi in enumerate([first, second, third, me]):
-            c0 = PC * gi
-            off = T.off1[:, c0 // 16:(c0 + PC) // 16]
+
+        def gather(p, c0, w, scalar, packs=None):
+            off = T.off1[:, c0 // 16:(c0 + w) // 16]
             for t in range(4):
-                o = T.xg[:, 4 * c0 + t:4 * (c0 + PC):4]
+                o = T.xg[:, 4 * c0 + t:4 * (c0 + w):4]
                 i = T.xb[:, t:4 * TOK].indirect(off)
-                if t < 2 + p % 2:
-                    C.activation(o, i, F.Copy).then_inc(S["gx%d" % p], 1)
-                else:
-                    V.tensor_copy(o, i).then_inc(S["gx%d" % p], 1)
-            if p == 1:
+                (C.activation(o, i, F.Copy) if t < scalar else V.tensor_copy(o, i)).then_inc(S["gx%d" % p], 1)
+            V.wait_ge(S["gx%d" % p], 4)
+            packs = packs or [("x", c0, c0, w)]
+            for dst, at, lo, k in packs:
+                V.quantize_mx(T[dst + "q"][:, at:at + k], T[dst + "s_"][:, at:at + k],
+                              T.xg[:, 4 * lo:4 * (lo + k)]).then_inc(S["q1_%d" % p], 1)
+            g.wait_ge(S["q1_%d" % p], len(packs))
+
+        direct = groups[by[1]] + groups[by[2]]
+        for f in range(2):
+            c0 = (HA + B) * f
+            if f:
                 V.wait_ge(S["ld_w"], 16)
                 V.quantize_mx(T.wq[:, 128:512], T.ws_[:, 128:512], T.wb[:, 512:2048]).then_inc(S["wqr"], 1)
+            gather(2 * f, c0, B, 2 + 2 * f)
+            for code in (True, False):
+                send([move(mine, near if f else far + near, "x", c0, "r", B * f, B, code, ("viaq%d" if code else "vias%d") % f)])
+            if f:
                 g.wait_ge(S["wqr"], 1)
-                send([move(mine, near, "w", 128, "u", 128, 384, True, "inw")])
-            V.wait_ge(S["gx%d" % p], 4)
-            V.quantize_mx(T.xq[:, c0:c0 + PC], T.xs_[:, c0:c0 + PC], T.xg[:, 4 * c0:4 * (c0 + PC)]).then_inc(S["q1_%d" % p], 1)
-            g.wait_ge(S["q1_%d" % p], 1)
-            if p == 0:
-                send([move(mine, far + near, "x", c0, "r", 0, PC, True, "viaq")])
-                send([move(mine, far + near, "x", c0, "r", 0, PC, False, "vias")])
-            elif p < 3:
-                send(step1(groups[gi], far, "x", 0, True)
-                     + ([move(mine, near, "w", 0, "u", 0, 512, False, "inw")] if p == 1 else []))
-                send(step1(groups[gi], far, "x", 0, False))
-            else:
-                send(step1([sib], near, "x", 0, True))
-                send(step1([sib], near, "x", 0, False))
+                send([move(mine, eng, "w", 128 * i, "u", 128 * i, 128 if i else 512, i > 0, "inw")
+                      for i, eng in share(range(4), near)])
+            gather(2 * f + 1, c0 + B, PC, 2)
+            for code in (True, False):
+                send(step1(f, [(a, c0 + B + HB * j) for j, a in enumerate(direct)], far, "x", code))
+        gather(4, HA - B, PC, 3, [("a", HB * (6 * f + 3), HA - B + B * f, B) for f in range(2)])
+        for code in (True, False):
+            send([t for f in range(2)
+                  for t in step1(f, [(sib, HB * (6 * f + 3 + sib % 2))], near[n // 2 * f:n // 2 * (f + 1)], "a", code)])
         E.wait_ge(S["wq0"], 1)
         E.wait_ge(S["wqr"], 1)
         wq, ws = T.wq, T.ws_
 
-    heard = {order1(c).index(me): c for c in ring(me)}
-    for m, k in enumerate([heard[1], me, heard[2], heard[0]]):
-        if k == me and not helps:
-            E.wait_ge(S["q1_3"], 1)
-            q, sc, lo = T.xq, T.xs_, B * rank
-        else:
-            E.wait_ge(S["in1_%d" % k], 2 * n if k == me else n)
-            q, sc, lo = T.aq, T.as_, B * k
+    par = (rank + helps) % 2
+
+    def step2(f, cs, engines, code):
+        out = []
+        for c, eng in share(cs, engines):
+            b, d = groups[c][f], (c - me) % G
+            blk = 2 * (d - 1) + par if d else 6
+            at = B * blk + (HB * (rank % 2) if d or par != f else B)
+            out.append(move(T.cores[b], eng, "h", PC * f + HB * c, "b", at, HB, code, "in2_%d" % blk))
+        return out
+
+    for m, (f, j) in enumerate(((0, 0), (0, 1), (1, 1), (1, 0))):
+        odd = j and rank % 2 and not helps
+        lo = HB * (6 * f + (0 if j == 0 else 4 if odd else 2))
+        ks = [by[1], by[0]] if j == 0 else [me, by[2]] if odd else [by[2], me]
+        E.wait_ge(S["in1_%d" % (2 * f + j)], 2 * n if j and helps else n)
+        if j and not helps:
+            E.wait_ge(S["q1_4"], 2)
         if m >= 2:
-            E.wait_ge(S["rl%d" % (m - 2)], 4)
+            E.wait_ge(S["rl%d" % (m - 2)], 8)
         base = 2048 * (m % 2)
         for i in (0, 2, 1, 3):
             E.matmul_mx(T.ps[:, base + 512 * i:base + 512 * i + B], wq[:, 128 * i:128 * i + 128],
-                        ws[:, 128 * i:128 * i + 128], q[:, lo:lo + B], sc[:, lo:lo + B],
-                        True, True).then_inc(S[("ma%d" if i < 2 else "mb%d") % m], 1)
-        C.wait_ge(S["ma%d" % m], 2)
-        V.wait_ge(S["mb%d" % m], 2)
+                        ws[:, 128 * i:128 * i + 128], T.aq[:, lo:lo + B], T.as_[:, lo:lo + B],
+                        True, True).then_inc(S["m%d_%d" % (i, m)], 1)
         for i in range(4):
-            o = T.h[:, 4 * k + i:4 * HA:16]
-            z = T.ps[:, base + 512 * i:base + 512 * i + B]
-            if i < 2:
-                C.activation(o, z, F.Relu, scale=0.043).then_inc(S["rl%d" % m], 1)
+            (C if i < 2 else V).wait_ge(S["m%d_%d" % (i, m)], 1)
+            for u, k in enumerate(ks):
+                o = T.h[:, 4 * PC * f + 4 * k + i:4 * PC * (f + 1):16]
+                z = T.ps[:, base + 512 * i + HB * u:base + 512 * i + HB * (u + 1)]
+                if i < 2:
+                    C.activation(o, z, F.Relu, scale=0.043).then_inc(S["rl%d" % m], 1)
+                else:
+                    V.tensor_scalar(o, z, 0.0, 0.043, A.max, A.mult).then_inc(S["rl%d" % m], 1)
+        if m % 2 == 0:
+            continue
+        for u in (m - 1, m):
+            V.wait_ge(S["rl%d" % u], 8)
+        c0 = PC * f
+        V.quantize_mx(T.hq[:, c0:c0 + PC], T.hs_[:, c0:c0 + PC], T.h[:, 4 * c0:4 * (c0 + PC)]).then_inc(S["q2_%d" % f], 1)
+        g.wait_ge(S["q2_%d" % f], 1)
+        for code in (True, False):
+            here = step2(f, [me], near, code) if helps or rank % 2 != f else []
+            if f == 0:
+                one, two = (far[:n // 2], far[n // 2:]) if code else (far[n // 2:], far[:n // 2])
+                send(step2(f, by[0:2], one, code) + step2(f, by[2:3], two, code) + here)
             else:
-                V.tensor_scalar(o, z, 0.0, 0.043, A.max, A.mult).then_inc(S["rl%d" % m], 1)
-    for m in range(4):
-        V.wait_ge(S["rl%d" % m], 4)
-    by = ring(me) + [me]
-    for p in range(G):
-        c0 = B * by[p]
-        V.quantize_mx(T.hq[:, c0:c0 + B], T.hs_[:, c0:c0 + B], T.h[:, 4 * c0:4 * (c0 + B)]).then_inc(S["q2_%d" % p], 1)
-
-    par = (rank + helps) % 2
-
-    def landing(b):
-        d = (b // 2 - me) % G
-        if d:
-            blk = 2 * (d - 1) + par
-            return blk, B * blk + HB * (rank % 2)
-        return 6, B * 6 + (HB * (rank % 2) if par != b % 2 else B)
-
-    def step2(ranks, engines, code):
-        return [move(T.cores[b], eng, "h", HB * b, "b", landing(b)[1], HB, code, "in2_%d" % landing(b)[0])
-                for b, eng in share(ranks, engines)]
-
-    here = groups[me] if helps else [sib]
-    for p in (0, 1):
-        g.wait_ge(S["q2_%d" % p], 1)
-    for code in (True, False):
-        send(step2(groups[by[0]] + groups[by[1]], far, code))
-    for p in (2, 3):
-        g.wait_ge(S["q2_%d" % p], 1)
-    for code in (True, False):
-        send(step2(groups[by[2]], far, code) + step2(here, near[:len(here) * n // 2], code))
+                send(step2(f, by[0:2], far, code) + here)
+        if f:
+            for code in (True, False):
+                send(step2(f, by[2:3], far, code))
     if helps:
         g.wait_ge(S["ls"], left[0])
         return
@@ -234,6 +246,8 @@ def rank_program(g, core, T, topo):
         V.tensor_copy(T.off2[32 * k:32 * k + 32, :], t[3]).then_inc(S["off2r"], 1)
 
     E.wait_ge(S["vqr"], 1)
+    for m in (2, 3):
+        E.wait_ge(S["rl%d" % m], 8)
     bank = [0]
     copied = [0]
 
@@ -247,26 +261,29 @@ def rank_program(g, core, T, topo):
             (V.tensor_copy(y, z) if on is V else C.activation(y, z, F.Copy)).then_inc(S["fc"], 1)
             copied[0] += 1
 
-    E.wait_ge(S["q2_3"], 1)
-    product(T.hq, T.hs_, B * me, B, C, [(HB * par, HB, HA * par + HB * rank)])
+    E.wait_ge(S["q2_%d" % par], 1)
+    product(T.hq, T.hs_, PC * par + B * (me // 2), B, C, [(HB * (me % 2), HB, HA * par + HB * rank)])
+    E.wait_ge(S["in2_6"], 6 * n)
+    product(T.bq, T.bs_, 6 * B, B + HB, V, [(0, B, HA * (1 - par) + B * me), (B, HB, HA * par + HB * sib)])
     for d in range(1, G):
-        if d == G - 1:
-            E.wait_ge(S["in2_6"], 3 * n)
-            product(T.bq, T.bs_, 6 * B, B + HB, V, [(0, B, HA * (1 - par) + B * me), (B, HB, HA * par + HB * sib)])
         for f in range(2):
             blk = 2 * (d - 1) + f
-            E.wait_ge(S["in2_%d" % blk], n if d < G - 1 else 2 * n)
+            E.wait_ge(S["in2_%d" % blk], (1 + par) * (n if d < G - 1 else 2 * n))
             product(T.bq, T.bs_, B * blk, B, (C, V)[f], [(0, B, HA * f + B * ((me - d) % G))])
-    H = TOK // 2
+    Q = TOK // 4
     for q in (C, V):
         q.wait_ge(S["off2r"], 4)
         q.wait_ge(S["fc"], copied[0])
-    C.activation(T.yt[:, 0:H], T.yv[:].indirect(T.off2[:, 0:H // 16]), F.Copy).then_inc(S["yv0"], 1)
-    V.tensor_copy(T.yt[:, H:TOK], T.yv[:].indirect(T.off2[:, H // 16:TOK // 16])).then_inc(S["yv1"], 1)
-    C.wait_ge(S["yv0"], 1)
-    C.dma_start(T.y[:, 0:H], T.yt[:, 0:H]).then_inc(S["st0"], 16)
-    g.sync.wait_ge(S["yv1"], 1)
-    g.sync.dma_start(T.y[:, H:TOK], T.yt[:, H:TOK]).then_inc(S["st1"], 16)
+
+    def part(u):
+        return T.yt[:, Q * u:Q * (u + 1)], T.yv[:].indirect(T.off2[:, Q * u // 16:Q * (u + 1) // 16])
+
+    for u in range(2):
+        C.activation(*part(u), F.Copy).then_inc(S["ya%d" % u], 1)
+        V.tensor_copy(*part(2 + u)).then_inc(S["yb%d" % u], 1)
+    for q, sem, u, st in ((g.sync, "ya0", 0, "st1"), (g.sync, "yb0", 2, "st1"), (C, "ya1", 1, "st0"), (g.sync, "yb1", 3, "st1")):
+        q.wait_ge(S[sem], 1)
+        q.dma_start(T.y[:, Q * u:Q * (u + 1)], T.yt[:, Q * u:Q * (u + 1)]).then_inc(S[st], 16)
     C.wait_ge(S["st0"], 16)
-    g.sync.wait_ge(S["st1"], 16)
+    g.sync.wait_ge(S["st1"], 48)
     g.wait_ge(S["ls"], left[0])

@@ -7,11 +7,12 @@ ALL = N * B
 HB = B // 2
 HA = ALL // 2
 PC = 2 * B
+PAIR, VIA, OWN = (0, 6), (2, 5), 3
 CODES, PLANE = "float8_e4m3fn_x4", "uint8"
 
 SCRATCH = {
-    "trib": ("sbuf", [128, ALL // 16], "int32"),
-    "off1": ("sbuf", [128, ALL // 16], "uint16"),
+    "trib": ("sbuf", [128, N, 2, N // 2], "int32"),
+    "off1": ("sbuf", [128, (ALL + PC) // 16], "uint16"),
     "pltb": ("sbuf", [128, TOK // 16], "int32"),
     "off2": ("sbuf", [128, TOK // 16], "uint16"),
     "xb": ("sbuf", [128, 4 * TOK], "bfloat16"),
@@ -23,16 +24,15 @@ SCRATCH = {
     "yt": ("sbuf", [128, TOK], "float32"),
     "ps": ("psum", [128, 4096], "float32"),
 }
-for _name, _cols in (("w", 512), ("v", 128), ("x", ALL), ("h", HA), ("u", 512), ("r", PC), ("a", 12 * HB),
-                     ("b", ALL - HB)):
+for _name, _cols in (("w", 512), ("v", 128), ("x", ALL), ("h", HA), ("u", 512), ("r", PC), ("a", HA), ("b", ALL)):
     SCRATCH[_name + "q"] = ("sbuf", [128, _cols], CODES)
     SCRATCH[_name + "s_"] = ("sbuf", [128, _cols], PLANE)
 for _f in range(4):
     SCRATCH["n%d" % _f] = ("sbuf", [128, TOK // 16], "int32")
 SEMAPHORES = (["ld_tri", "ld_x", "ld_w", "ld_w0", "wq0", "ld_v", "ld_plt", "off0r", "off1r", "off2r", "wqr", "vqr", "pt",
                "ls", "fc", "ya0", "ya1", "yb0", "yb1", "st0", "st1", "viaq0", "viaq1", "vias0", "vias1", "inw"]
-              + [s + "%d" % p for p in range(5) for s in ("gx", "q1_", "q2_", "in1_", "rl", "m0_", "m1_", "m2_", "m3_")]
-              + ["in2_%d" % p for p in range(7)] + ["fm%d" % k for k in range(8)])
+              + [s + "%d" % p for p in range(7) for s in ("gx", "q1_", "q2_", "in1_", "rl", "m0_", "m1_", "m2_", "m3_")]
+              + ["in2_%d" % p for p in range(8)] + ["fm%d" % k for k in range(8)])
 
 
 def bits(engines):
@@ -66,8 +66,11 @@ def rank_program(g, core, T, topo):
     me = chips.index(topo.chip(core))
     G = len(groups)
     sib = [r for r in groups[me] if r != rank][0]
-    by = [(me + d) % G for d in range(1, G + 1)]
-    far = topo.engines(core, T.cores[groups[by[0]][0]])
+    partner = [c for c in range(G) if c != me and c // 2 == me // 2][0]
+    rest = [c for c in range(G) if c // 2 != me // 2]
+    longer = sorted(rest, key=lambda c: topo.same_plane(chips[me], chips[c]))
+    half = (1 - me // 2, me // 2)
+    far = topo.engines(core, T.cores[groups[partner][0]])
     near = [e for e in topo.engines(core, T.cores[sib]) if e not in far]
     n = len(far)
 
@@ -92,25 +95,22 @@ def rank_program(g, core, T, topo):
     def send(moves):
         g.remote_dma_fused(moves, local_sem=S["ls"])
 
-    def step1(f, items, engines, src, code):
-        out = []
-        for (a, lo), eng in share(items, engines):
-            d = (a // 2 - me) % G
-            place = d - 2 if d > 1 else 3 if d == 0 else 5 if a % 2 and rank % 2 else 2
-            out.append(move(worker(rank, a), eng, src, lo, "a", HB * (6 * f + place), HB, code, "in1_%d" % (2 * f + (d < 2))))
-        return out
+    def direct(f, cs, code):
+        return [move(worker(rank, a), eng, "x", HA * f + HB * a, "a", HB * (PAIR[f] + me % 2), HB, code, "in1_%d" % (2 * f))
+                for a, eng in share([a for c in cs for a in groups[c]], far)]
 
     if helps:
         for f in range(2):
             for code in (True, False):
-                g.wait_ge(S[("viaq%d" if code else "vias%d") % f], n if f else 2 * n)
-                send(step1(f, [(a, B * f + HB * (a % 2)) for a in groups[by[0]]], far, "r", code))
-        E.wait_ge(S["inw"], 3 * n)
+                g.wait_ge(S[("viaq%d" if code else "vias%d") % f], 2 * n if code and f == 0 else n)
+                send([move(worker(rank, a), eng, "r", B * f + HB * (a % 2), "a", HB * VIA[f], HB, code, "in1_%d" % (2 * f + 1))
+                      for a, eng in share(groups[partner], far if f else far[:n // 2] if code else far[n // 2:])])
+        E.wait_ge(S["inw"], 4 * n)
         wq, ws = T.uq, T.us_
     else:
+        for k, q in enumerate((C, g.sync)):
+            q.dma_start(T.trib[16 * k:16 * k + 16], T.tri[:]).then_inc(S["ld_tri"], 16)
         g.sync.dma_start(T.wb[:, 0:512], T.w[:, 0:512]).then_inc(S["ld_w0"], 16)
-        for k in range(2):
-            C.dma_start(T.trib[16 * k:16 * k + 16, :], T.tri[:]).then_inc(S["ld_tri"], 16)
         g.sync.dma_start(T.xb[:], T.x[:]).then_inc(S["ld_x"], 16)
         g.sync.dma_start(T.wb[:, 512:2048], T.w[:, 512:2048]).then_inc(S["ld_w"], 16)
         g.sync.dma_start(T.vb[:], T.vv[:]).then_inc(S["ld_v"], 16)
@@ -118,115 +118,113 @@ def rank_program(g, core, T, topo):
             g.sync.dma_start(T.pltb[16 * k:16 * k + 16, :], T.plt[:]).then_inc(S["ld_plt"], 16)
 
         mine = helper(rank, T, topo)
-        V.wait_ge(S["ld_w0"], 16)
-        V.quantize_mx(T.wq[:, 0:128], T.ws_[:, 0:128], T.wb[:, 0:512]).then_inc(S["wq0"], 1)
         g.wait_ge(S["wq0"], 1)
-        send([move(mine, far + near, "w", 0, "u", 0, 128, True, "inw")])
+        for j, eng in enumerate((near, far)):
+            send([move(mine, eng, "w", 64 * j, "u", 64 * j, 64, True, "inw")])
 
         V.wait_ge(S["ld_tri"], 32)
-        made = 0
-        for f, c0 in enumerate((by[0], me)):
-            for lo, hi in ((c0, G), (0, c0)):
-                if hi > lo:
-                    to = 32 * f + 8 * ((lo - c0) % G)
-                    V.tensor_scalar(T.off1[0:32, to:to + 8 * (hi - lo)], T.trib[0:32, 16 * lo + f:16 * hi:2],
-                                    4.0, 0.0, A.mult, A.max).then_inc(S["off0r"], 1)
-                    made += 1
-        V.wait_ge(S["off0r"], made)
+        runs = [(32 * f + 16 * k, 16, T.trib[0:32, 4 * k:4 * k + 4, k if f else 1 - k, :]) for f in range(2) for k in range(2)]
+        runs.append((64, 16, T.trib[0:32, 2 * me:2 * me + 2, :, :]))
+        for j, (to, k, lists) in enumerate(runs):
+            if j == 3:
+                V.wait_ge(S["ld_w0"], 16)
+                V.quantize_mx(T.wq[:, 0:128], T.ws_[:, 0:128], T.wb[:, 0:512]).then_inc(S["wq0"], 1)
+            V.tensor_scalar(T.off1[0:32, to:to + k], lists, 4.0, 0.0, A.mult, A.max).then_inc(S["off0r"], 1)
+        V.wait_ge(S["off0r"], len(runs))
         for k in range(1, 4):
             V.tensor_copy(T.off1[32 * k:32 * k + 32, :], T.off1[0:32, :]).then_inc(S["off1r"], 1)
         for q in (V, C):
             q.wait_ge(S["off1r"], 3)
             q.wait_ge(S["ld_x"], 16)
 
-        def gather(p, c0, w, scalar, packs=None):
-            off = T.off1[:, c0 // 16:(c0 + w) // 16]
+        def gather(p, c0, w, scalar, lists=None, dst="x", at=None):
+            lists = c0 if lists is None else lists
+            off = T.off1[:, lists // 16:(lists + w) // 16]
             for t in range(4):
                 o = T.xg[:, 4 * c0 + t:4 * (c0 + w):4]
                 i = T.xb[:, t:4 * TOK].indirect(off)
                 (C.activation(o, i, F.Copy) if t < scalar else V.tensor_copy(o, i)).then_inc(S["gx%d" % p], 1)
             V.wait_ge(S["gx%d" % p], 4)
-            packs = packs or [("x", c0, c0, w)]
-            for dst, at, lo, k in packs:
-                V.quantize_mx(T[dst + "q"][:, at:at + k], T[dst + "s_"][:, at:at + k],
-                              T.xg[:, 4 * lo:4 * (lo + k)]).then_inc(S["q1_%d" % p], 1)
-            g.wait_ge(S["q1_%d" % p], len(packs))
+            at = c0 if at is None else at
+            V.quantize_mx(T[dst + "q"][:, at:at + w], T[dst + "s_"][:, at:at + w],
+                          T.xg[:, 4 * c0:4 * (c0 + w)]).then_inc(S["q1_%d" % p], 1)
+            g.wait_ge(S["q1_%d" % p], 1)
 
-        direct = groups[by[1]] + groups[by[2]]
         for f in range(2):
-            c0 = (HA + B) * f
+            c0 = HA * f + B * partner
+            gather(3 * f, c0, B, 2)
+            send([move(mine, near if f else far + near, "x", c0, "r", B * f, B, True, "viaq%d" % f)])
+            send([move(mine, near, "x", c0, "r", B * f, B, False, "vias%d" % f)])
             if f:
+                send([move(mine, near, "w", 256, "u", 256, 256, True, "inw")])
+                gather(4, HA + B * rest[0], PC, 2)
+                send(direct(f, rest, True))
+            else:
+                gather(1, B * longer[0], B, 2)
+                send(direct(f, longer[:1], True))
                 V.wait_ge(S["ld_w"], 16)
                 V.quantize_mx(T.wq[:, 128:512], T.ws_[:, 128:512], T.wb[:, 512:2048]).then_inc(S["wqr"], 1)
-            gather(2 * f, c0, B, 2 + 2 * f)
-            for code in (True, False):
-                send([move(mine, near if f else far + near, "x", c0, "r", B * f, B, code, ("viaq%d" if code else "vias%d") % f)])
-            if f:
                 g.wait_ge(S["wqr"], 1)
                 send([move(mine, eng, "w", 128 * i, "u", 128 * i, 128 if i else 512, i > 0, "inw")
-                      for i, eng in share(range(4), near)])
-            gather(2 * f + 1, c0 + B, PC, 2)
-            for code in (True, False):
-                send(step1(f, [(a, c0 + B + HB * j) for j, a in enumerate(direct)], far, "x", code))
-        gather(4, HA - B, PC, 3, [("a", HB * (6 * f + 3), HA - B + B * f, B) for f in range(2)])
+                      for i, eng in share(range(2), near)])
+                gather(2, B * longer[1], B, 4)
+                send(direct(f, longer[1:], True))
+            send(direct(f, rest, False))
+        gather(5, B * me, B, 3, ALL + B * (sib % 2))
         for code in (True, False):
-            send([t for f in range(2)
-                  for t in step1(f, [(sib, HB * (6 * f + 3 + sib % 2))], near[n // 2 * f:n // 2 * (f + 1)], "a", code)])
+            send([move(worker(rank, sib), near, "x", B * me, "a", HB * OWN, B, code, "in1_4")])
+        gather(6, HA + B * me, B, 2, ALL + B * (rank % 2), "a", HB * OWN)
         E.wait_ge(S["wq0"], 1)
         E.wait_ge(S["wqr"], 1)
         wq, ws = T.wq, T.ws_
 
     par = (rank + helps) % 2
 
-    def step2(f, cs, engines, code):
+    def step2(f, ranks, engines, code):
         out = []
-        for c, eng in share(cs, engines):
-            b, d = groups[c][f], (c - me) % G
-            blk = 2 * (d - 1) + par if d else 6
-            at = B * blk + (HB * (rank % 2) if d or par != f else B)
-            out.append(move(T.cores[b], eng, "h", PC * f + HB * c, "b", at, HB, code, "in2_%d" % blk))
+        for b, eng in share(ranks, engines):
+            blk = 2 * me + (par if b // 2 != me else 0)
+            at = B * blk + (HB * (rank % 2) if b // 2 != me or par != b % 2 else B)
+            out.append(move(T.cores[b], eng, "h", PC * f + HB * (b % 4), "b", at, HB, code, "in2_%d" % blk))
         return out
 
-    for m, (f, j) in enumerate(((0, 0), (0, 1), (1, 1), (1, 0))):
-        odd = j and rank % 2 and not helps
-        lo = HB * (6 * f + (0 if j == 0 else 4 if odd else 2))
-        ks = [by[1], by[0]] if j == 0 else [me, by[2]] if odd else [by[2], me]
-        E.wait_ge(S["in1_%d" % (2 * f + j)], 2 * n if j and helps else n)
-        if j and not helps:
-            E.wait_ge(S["q1_4"], 2)
+    own = [(("in1_4", 2 * n) if helps else ("q1_6", 1), OWN, [(OWN + half[f], f, me)]) for f in range(2)]
+    pair = [(("in1_%d" % (2 * f), (3 - f) * n // 2), PAIR[f], [(PAIR[f] + c % 2, f, c) for c in rest]) for f in range(2)]
+    via = [(("in1_%d" % (2 * f + 1), (1 + f) * n // 2), VIA[f] - 1, [(VIA[f], f, partner)]) for f in range(2)]
+    work = ([pair[0], own[0], via[0], own[1]] if helps else [own[0], own[1], pair[0], via[0]]) + [via[1], pair[1]]
+    for m, ((sem, count), lo, sources) in enumerate(work):
+        E.wait_ge(S[sem], count)
         if m >= 2:
-            E.wait_ge(S["rl%d" % (m - 2)], 8)
+            E.wait_ge(S["rl%d" % (m - 2)], 4 * len(work[m - 2][2]))
         base = 2048 * (m % 2)
         for i in (0, 2, 1, 3):
             E.matmul_mx(T.ps[:, base + 512 * i:base + 512 * i + B], wq[:, 128 * i:128 * i + 128],
-                        ws[:, 128 * i:128 * i + 128], T.aq[:, lo:lo + B], T.as_[:, lo:lo + B],
+                        ws[:, 128 * i:128 * i + 128], T.aq[:, HB * lo:HB * lo + B], T.as_[:, HB * lo:HB * lo + B],
                         True, True).then_inc(S["m%d_%d" % (i, m)], 1)
         for i in range(4):
             (C if i < 2 else V).wait_ge(S["m%d_%d" % (i, m)], 1)
-            for u, k in enumerate(ks):
+            for place, f, k in sources:
                 o = T.h[:, 4 * PC * f + 4 * k + i:4 * PC * (f + 1):16]
-                z = T.ps[:, base + 512 * i + HB * u:base + 512 * i + HB * (u + 1)]
+                z = T.ps[:, base + 512 * i + HB * (place - lo):base + 512 * i + HB * (place - lo + 1)]
                 if i < 2:
                     C.activation(o, z, F.Relu, scale=0.043).then_inc(S["rl%d" % m], 1)
                 else:
                     V.tensor_scalar(o, z, 0.0, 0.043, A.max, A.mult).then_inc(S["rl%d" % m], 1)
-        if m % 2 == 0:
+        if work[m] not in (via[0], pair[1]):
             continue
-        for u in (m - 1, m):
-            V.wait_ge(S["rl%d" % u], 8)
-        c0 = PC * f
-        V.quantize_mx(T.hq[:, c0:c0 + PC], T.hs_[:, c0:c0 + PC], T.h[:, 4 * c0:4 * (c0 + PC)]).then_inc(S["q2_%d" % f], 1)
-        g.wait_ge(S["q2_%d" % f], 1)
-        for code in (True, False):
-            here = step2(f, [me], near, code) if helps or rank % 2 != f else []
-            if f == 0:
-                one, two = (far[:n // 2], far[n // 2:]) if code else (far[n // 2:], far[:n // 2])
-                send(step2(f, by[0:2], one, code) + step2(f, by[2:3], two, code) + here)
-            else:
-                send(step2(f, by[0:2], far, code) + here)
-        if f:
-            for code in (True, False):
-                send(step2(f, by[2:3], far, code))
+        for u in range(m + 1):
+            if work[u][2][0][1] == f:
+                V.wait_ge(S["rl%d" % u], 4 * len(work[u][2]))
+        for c in ([partner, me] if f else longer):
+            c0 = PC * f + B * (c % 2)
+            V.quantize_mx(T.hq[:, c0:c0 + B], T.hs_[:, c0:c0 + B], T.h[:, 4 * c0:4 * (c0 + B)]).then_inc(S["q2_%d" % c], 1)
+            if c != me:
+                g.wait_ge(S["q2_%d" % c], 1)
+                send(step2(f, groups[c], far, True))
+        send(step2(f, groups[partner] if f else groups[rest[0]] + groups[rest[1]], far, False))
+    g.wait_ge(S["q2_%d" % me], 1)
+    for code in (True, False):
+        send(step2(1, groups[me], near, code) if helps else step2(1, [sib], near[:n // 2], code))
     if helps:
         g.wait_ge(S["ls"], left[0])
         return
@@ -246,8 +244,8 @@ def rank_program(g, core, T, topo):
         V.tensor_copy(T.off2[32 * k:32 * k + 32, :], t[3]).then_inc(S["off2r"], 1)
 
     E.wait_ge(S["vqr"], 1)
-    for m in (2, 3):
-        E.wait_ge(S["rl%d" % m], 8)
+    for m in (4, 5):
+        E.wait_ge(S["rl%d" % m], 4 * len(work[m][2]))
     bank = [0]
     copied = [0]
 
@@ -261,15 +259,16 @@ def rank_program(g, core, T, topo):
             (V.tensor_copy(y, z) if on is V else C.activation(y, z, F.Copy)).then_inc(S["fc"], 1)
             copied[0] += 1
 
-    E.wait_ge(S["q2_%d" % par], 1)
-    product(T.hq, T.hs_, PC * par + B * (me // 2), B, C, [(HB * (me % 2), HB, HA * par + HB * rank)])
-    E.wait_ge(S["in2_6"], 6 * n)
-    product(T.bq, T.bs_, 6 * B, B + HB, V, [(0, B, HA * (1 - par) + B * me), (B, HB, HA * par + HB * sib)])
-    for d in range(1, G):
+    E.wait_ge(S["q2_%d" % me], 1)
+    product(T.hq, T.hs_, PC + B * (me % 2), B, C, [(HB * par, HB, HA * par + HB * rank)])
+    for c in longer + [me, partner]:
+        if c == me:
+            E.wait_ge(S["in2_%d" % (2 * c)], 3 * n)
+            product(T.bq, T.bs_, PC * c, B + HB, V, [(0, B, HA * (1 - par) + B * c), (B, HB, HA * par + HB * sib)])
+            continue
         for f in range(2):
-            blk = 2 * (d - 1) + f
-            E.wait_ge(S["in2_%d" % blk], (1 + par) * (n if d < G - 1 else 2 * n))
-            product(T.bq, T.bs_, B * blk, B, (C, V)[f], [(0, B, HA * f + B * ((me - d) % G))])
+            E.wait_ge(S["in2_%d" % (2 * c + f)], 2 * n if c == partner else 3 * n // 2)
+            product(T.bq, T.bs_, PC * c + B * f, B, (C, V)[f], [(0, B, HA * f + B * c)])
     Q = TOK // 4
     for q in (C, V):
         q.wait_ge(S["off2r"], 4)

@@ -1,18 +1,35 @@
 from concourse.bass import DstId, RemoteDMATransfer
 from concourse.mybir import AluOpType, ActivationFunctionType, dt
 
+OUT = ("!D a:D !Y a:Y b:D,Y", "!D !Y b:D,Y a:D a:Y")
+END = " !S a:S b:S !X a:X b:X"
+OPT = dict(
+    R=("G2:S0r,Y0r s:S0r,Y0r q:S0r,Y0r G2:S0h,Y0h q:S0h,Y0h s:S0h,Y0h W G3:D0r,D0h q:D0r,D0h s:D0r,D0h "
+       "G2J:D1r,D1h G0:Y1r,Y1h Q:D1 P:D1 q:Y1r,Y1h G3:X0r,X0h q:X0h s:Y1r,Y1h,X0h G3:S1r,S1h q:S1r,S1h s:S1r,S1h "
+       "G3:X1r,X1h q:X1h s:X1h *X0+Y0 *D0+S0 !D a:D b:D !Y a:Y b:Y *X1+Y1 *D1+S1" + END,) * 2,
+    H=("s:S0r q:S0r,S0h s:S0h q:D1r,D1h s:D1r,D1h *Y0+D0 *X0+S0 !D a:D b:D !Y a:Y b:Y *Y1+X1 *D1+S1" + END,) * 2,
+    last="DYXS",
+    weng="nfnn",
+    halves="plane",
+    both=(),
+    flip=("qS1", "QD1", "qD1", "aS", "aY", "aD"),
+    wat=0,
+    one=1,
+    evac=dict(R=[2, 2, 3, 2], H=[2, 2, 3, 2]),
+    cut=(1, 2),
+    hsplit=(),
+)
 N, TOK, TR = 8, 512, 16
 B = N * TR
 ALL = N * B
 HB = B // 2
 HA = ALL // 2
 PC = 2 * B
-PAIR, VIA, OWN = (0, 6), (2, 5), 3
 CODES, PLANE = "float8_e4m3fn_x4", "uint8"
 
 SCRATCH = {
-    "trib": ("sbuf", [128, N, 2, N // 2], "int32"),
-    "off1": ("sbuf", [128, (ALL + PC) // 16], "uint16"),
+    "trib": ("sbuf", [128, N // 2, 2, N // 2, 2], "int32"),
+    "off1": ("sbuf", [128, ALL // 16], "uint16"),
     "pltb": ("sbuf", [128, TOK // 16], "int32"),
     "off2": ("sbuf", [128, TOK // 16], "uint16"),
     "xb": ("sbuf", [128, 4 * TOK], "bfloat16"),
@@ -24,62 +41,123 @@ SCRATCH = {
     "yt": ("sbuf", [128, TOK], "float32"),
     "ps": ("psum", [128, 4096], "float32"),
 }
-for _name, _cols in (("w", 512), ("v", 128), ("x", ALL), ("h", HA), ("u", 512), ("r", PC), ("a", HA), ("b", ALL)):
+for _name, _cols in (("w", 512), ("v", 128), ("x", ALL), ("h", HA), ("u", 512), ("r", ALL), ("a", 10 * HB), ("b", ALL)):
     SCRATCH[_name + "q"] = ("sbuf", [128, _cols], CODES)
     SCRATCH[_name + "s_"] = ("sbuf", [128, _cols], PLANE)
 for _f in range(4):
     SCRATCH["n%d" % _f] = ("sbuf", [128, TOK // 16], "int32")
 SEMAPHORES = (["ld_tri", "ld_x", "ld_w", "ld_w0", "wq0", "ld_v", "ld_plt", "off0r", "off1r", "off2r", "wqr", "vqr", "pt",
-               "ls", "fc", "ya0", "ya1", "yb0", "yb1", "st0", "st1", "viaq0", "viaq1", "vias0", "vias1", "inw"]
-              + [s + "%d" % p for p in range(7) for s in ("gx", "q1_", "q2_", "in1_", "rl", "m0_", "m1_", "m2_", "m3_")]
-              + ["in2_%d" % p for p in range(8)] + ["fm%d" % k for k in range(8)])
+               "ls", "fc", "yh0", "yh1", "st1", "inw"]
+              + [s + p + f for p in "DYS" for f in "01" for s in ("onqr", "onqh", "onsr", "onsh")]
+              + ["in1_" + p + f for p in "DYSX" for f in "01"] + ["q2_" + p for p in "DYSX"]
+              + [s + "%d" % p for p in range(8) for s in ("gx", "q1_", "rl", "m0_", "m1_", "m2_", "m3_", "in2_", "fm")])
 
 
 def bits(engines):
     return sum(1 << e for e in engines)
 
 
-def helper(r, T, topo):
-    c = T.cores[r]
-    free = [o for o in topo.cores_of(c) if topo.die(o) != topo.die(c) and T.rank_of(o) is None
-            and all(topo.may_write(o, d) for d in T.cores if topo.chip(d) != topo.chip(c))]
-    return free[[d for d in T.cores if topo.chip(d) == topo.chip(c)].index(c)]
-
-
 def rank_program(g, core, T, topo):
-    rank = T.rank_of(core)
-    helps = rank is None
-    if helps:
-        served = [r for r in range(N) if helper(r, T, topo) == core]
-        if not served:
-            return
-        rank = served[0]
-    S = T.sem
-    A = AluOpType
-    F = ActivationFunctionType
-    V, E, C = g.vector, g.tensor, g.scalar
     chips = []
     for c in T.cores:
         if topo.chip(c) not in chips:
             chips.append(topo.chip(c))
     groups = [[r for r in range(N) if topo.chip(T.cores[r]) == c] for c in chips]
-    me = chips.index(topo.chip(core))
     G = len(groups)
+
+    def plane(m):
+        return [c for c in range(G) if c == m or topo.same_plane(chips[m], chips[c])]
+
+    def helper(r):
+        c = T.cores[r]
+        return [o for o in topo.cores_of(c) if T.rank_of(o) is None and all(topo.may_write(o, d) for d in T.cores)][r % 2]
+
+    rank, kind = T.rank_of(core), "R"
+    if rank is None:
+        served = [r for r in range(N) if helper(r) == core]
+        if not served:
+            return
+        rank, kind = served[0], "H"
+    me, odd = rank // 2, rank % 2
     sib = [r for r in groups[me] if r != rank][0]
-    partner = [c for c in range(G) if c != me and c // 2 == me // 2][0]
-    rest = [c for c in range(G) if c // 2 != me // 2]
-    longer = sorted(rest, key=lambda c: topo.same_plane(chips[me], chips[c]))
-    half = (1 - me // 2, me // 2)
-    far = topo.engines(core, T.cores[groups[partner][0]])
-    near = [e for e in topo.engines(core, T.cores[sib]) if e not in far]
+    other = [c for c in range(G) if c not in plane(me)]
+    k = plane(me).index(me)
+    chip = dict(D=other[k], Y=other[1 - k], S=plane(me)[1 - k], X=me)
+    own = plane(me) if OPT["halves"] == "plane" else sorted([me, chip["D"]])
+    halves = ([c for c in range(G) if c not in own], own)
+    S = T.sem
+    A = AluOpType
+    F = ActivationFunctionType
+    V, E, C = g.vector, g.tensor, g.scalar
+    aid = helper(rank)
+    every = topo.engines(core, T.cores[sib])
+    far = topo.engines(core, T.cores[groups[chip["D"]][0]])
+    near = [e for e in every if e not in far]
     n = len(far)
+    script = {k: [[p.split(":") for p in s.split()] for s in OPT[k]] for k in "RH"}
+    for k in "RH":
+        l = script[k][1]
+        for j in range(len(l) - 1):
+            if l[j][1:] == l[j + 1][1:] and l[j][0] + l[j + 1][0] in ("qs", "ab", "QP") and l[j][0] + l[j][1][:2] in OPT["flip"]:
+                l[j], l[j + 1] = l[j + 1], l[j]
+    handed = [set(u for p in s if p[0] in "qs" for u in p[1].split(",")) for s in script["H"]]
 
-    def worker(s, a):
-        return T.cores[a] if s % 2 == a % 2 else helper(a, T, topo)
+    def target(u):
+        return groups[chip[u[0]]][(rank + (u[2] == "h")) % 2]
 
-    def share(items, engines):
-        k = len(engines) // len(items)
-        return [(it, engines[k * i:k * (i + 1)]) for i, it in enumerate(items)]
+    def half_of(c, f):
+        return halves[f] if c in own else halves[1 - f]
+
+    def key(u):
+        return (chip[u[0]], target(u) % 2, half_of(chip[u[0]], int(u[1]))[0])
+
+    tiles = [[sorted(p[1].split(","), key=key) for p in s if p[0][0] == "G"] for s in script["R"]]
+
+    def calls(k, o):
+        out = []
+        for p in script[k][o]:
+            if p[0] in ("q", "s"):
+                us = p[1].split(",")
+                off = [u for u in us if k == "H" or (u not in handed[o] and u[0] != "X")]
+                on = [u for u in us if u not in off]
+                lo, m = OPT["hsplit"][len(out)] if k == "H" and len(out) < len(OPT["hsplit"]) else (0, n)
+                out.append((p, [(u, l is off, lo + j * (m // len(l)), m // len(l)) for l in (off, on) for j, u in enumerate(l)]))
+        return out
+
+    def arrivals(u):
+        o = (odd + (u[2] == "h")) % 2
+        return sum(w for k in "RH" for _, l in calls(k, o) for v, off, _, w in l if v == u and (k == "H" or u not in handed[o]))
+
+    def landed(u, code):
+        for p in script["R"][odd]:
+            if p[0] == "QP"[not code] and p[1] == u[:2]:
+                return "r", (2 * n if p[0] + p[1] in OPT["both"] else n)
+        return u[2], [w for p, l in calls("R", odd) for v, _, _, w in l if v == u and p[0] == "qs"[not code]][0]
+
+    def layout(k, o):
+        at, out = 0, {}
+        for p in script[k][o]:
+            if p[0][0] != "*":
+                continue
+            w = p[0][1:].split("+")
+            if k == "R" and w[0][0] == "X" and len(w) > 1 and w[1][0] != "X":
+                out[w[0]], out["tile" + w[0]] = at + (len(w) - 1 if o == 0 else 1), at + (len(w) - 1 if o == 0 else 0)
+                for j, s in enumerate(w[1:]):
+                    out[s] = at + j + 2 * o
+                at += len(w) + 1
+            for s in w:
+                if s in out:
+                    continue
+                if s[0] != "X" or k == "H":
+                    out[s] = at
+                    at += 1
+                    continue
+                for j, u in enumerate([t for t in tiles[o] if s + "r" in t][0]):
+                    if u[0] == "X" and u[2] == "r":
+                        out[u[:2]] = at + j
+                        out["tile" + u[:2]] = at
+                at += 2
+        return out
 
     left = [0]
 
@@ -95,137 +173,214 @@ def rank_program(g, core, T, topo):
     def send(moves):
         g.remote_dma_fused(moves, local_sem=S["ls"])
 
-    def direct(f, cs, code):
-        return [move(worker(rank, a), eng, "x", HA * f + HB * a, "a", HB * (PAIR[f] + me % 2), HB, code, "in1_%d" % (2 * f))
-                for a, eng in share([a for c in cs for a in groups[c]], far)]
+    def share(items, engines):
+        k = len(engines) // len(items)
+        return [(it, engines[k * i:k * (i + 1)]) for i, it in enumerate(items)]
 
-    if helps:
-        for f in range(2):
-            for code in (True, False):
-                g.wait_ge(S[("viaq%d" if code else "vias%d") % f], 2 * n if code and f == 0 else n)
-                send([move(worker(rank, a), eng, "r", B * f + HB * (a % 2), "a", HB * VIA[f], HB, code, "in1_%d" % (2 * f + 1))
-                      for a, eng in share(groups[partner], far if f else far[:n // 2] if code else far[n // 2:])])
-        E.wait_ge(S["inw"], 4 * n)
+    place = layout(kind, odd)
+    par = (rank + (kind == "H")) % 2
+
+    def source(u):
+        j = [j for j, t in enumerate(tiles[odd]) if u in t][0]
+        t = tiles[odd][j]
+        mine = [v for v in t if v[0] == "X" and v[2] == "r"]
+        at = B * j + HB * t.index(u)
+        if mine:
+            return j, "a", HB * (layout("R", odd)["tile" + mine[0][:2]] + t.index(u)), at
+        return j, "x", at, at
+
+    waited = []
+
+    def wait(q, sem, count):
+        if (q is g, q is V, sem) not in waited:
+            waited.append((q is g, q is V, sem))
+            q.wait_ge(S[sem], count)
+
+    def step1(p):
+        code = p[0] == "q"
+        out = []
+        for u, off, j, w in [l for q, l in calls(kind, odd) if q is p][0]:
+            tile, src, lo, at = source(u)
+            eng = (far if off else near)[j:j + w]
+            if kind == "H":
+                k, count = landed(u, code)
+                wait(g, ("onq" if code else "ons") + k + u[:2], count)
+                src, lo = "r", at
+            else:
+                wait(g, "q1_%d" % tile, 1)
+            if kind == "R" and u in handed[odd]:
+                out.append(move(aid, eng, src, lo, "r", at, HB, code, ("onq" if code else "ons") + u[2] + u[:2]))
+            else:
+                a = target(u)
+                out.append(move(T.cores[a] if u[2] == "r" else helper(a), eng, src, lo, "a",
+                                HB * layout(u[2].upper(), a % 2)[u[:2]], HB, code, "in1_" + u[:2]))
+        send(out)
+
+    def step2(p):
+        code = p[0] == "a"
+        cs = p[1].split(",")
+        out = []
+        for on in (False, True):
+            to = [b for c in cs for b in groups[chip[c]] if (c == "X") == on and T.cores[b] != core]
+            if not to:
+                continue
+            for b, eng in share(to, (near[:n // 2 * len(to)] if on else far)):
+                c = b // 2
+                blk = 2 * me + (par if c != me else 0)
+                at = B * blk + (HB * odd if c != me or par != b % 2 else B)
+                out.append(move(T.cores[b], eng, "h", column(c) + HB * (b % 2), "b", at, HB, code, "in2_%d" % blk))
+        for c in cs:
+            wait(g, "q2_" + c, 1)
+        send(out)
+
+    def weights(j):
+        eng = near if OPT["weng"][j] == "n" else far
+        if j < 2:
+            return [move(aid, eng[:n // OPT["cut"][j]], "w", 64 * j, "u", 64 * j, 64, True, "inw")]
+        if j == 3:
+            return [move(aid, eng, "w", 256, "u", 256, 256, True, "inw")]
+        return [move(aid, e, "w", 128 * i, "u", 128 * i, 128 if i else 512, i > 0, "inw")
+                for i, e in share(range(2 if ["w"] in script["R"][odd] else 4), eng)]
+
+    sorted_at = {}
+    if kind != "R":
+        E.wait_ge(S["inw"], (1 + (["w"] in script["R"][odd])) * n + (n // OPT["cut"][0] + n // OPT["cut"][1] if OPT["one"] != 2 else n))
         wq, ws = T.uq, T.us_
     else:
-        for k, q in enumerate((C, g.sync)):
-            q.dma_start(T.trib[16 * k:16 * k + 16], T.tri[:]).then_inc(S["ld_tri"], 16)
-        g.sync.dma_start(T.wb[:, 0:512], T.w[:, 0:512]).then_inc(S["ld_w0"], 16)
+        C.dma_start(T.wb[:, 0:512], T.w[:, 0:512]).then_inc(S["ld_w0"], 16)
+        for k in range(2):
+            g.sync.dma_start(T.trib[16 * k:16 * k + 16], T.tri[:]).then_inc(S["ld_tri"], 16)
         g.sync.dma_start(T.xb[:], T.x[:]).then_inc(S["ld_x"], 16)
         g.sync.dma_start(T.wb[:, 512:2048], T.w[:, 512:2048]).then_inc(S["ld_w"], 16)
         g.sync.dma_start(T.vb[:], T.vv[:]).then_inc(S["ld_v"], 16)
         for k in range(2):
             g.sync.dma_start(T.pltb[16 * k:16 * k + 16, :], T.plt[:]).then_inc(S["ld_plt"], 16)
 
-        mine = helper(rank, T, topo)
         g.wait_ge(S["wq0"], 1)
-        for j, eng in enumerate((near, far)):
-            send([move(mine, eng, "w", 64 * j, "u", 64 * j, 64, True, "inw")])
+        if OPT["one"] == 3:
+            send(weights(1))
+            send(weights(0))
+        else:
+            send(weights(0) + weights(1) if OPT["one"] == 1 else [move(aid, near, "w", 0, "u", 0, 128, True, "inw")])
 
+        def span(a, b):
+            return slice(a, b + 1, max(b - a, 1))
+
+        runs, todo = [], list(range(len(tiles[odd])))
+        while todo:
+            u, v = tiles[odd][todo[0]]
+            lists = span(*half_of(chip[u[0]], int(u[1])))
+            at = B * len(sorted_at)
+            if u[:2] != v[:2]:
+                runs += [(at + HB * k, HB, T.trib[0:32, chip[w[0]], target(w) % 2, span(*half_of(chip[w[0]], int(w[1]))), :])
+                         for k, w in enumerate((u, v))]
+                js = todo[:1]
+            else:
+                js = [j for j in todo if tiles[odd][j][0][:2] == tiles[odd][j][1][:2] and tiles[odd][j][0][1] == u[1]
+                      and (chip[tiles[odd][j][0][0]] in own) == (chip[u[0]] in own)]
+                js.sort(key=lambda j: chip[tiles[odd][j][0][0]])
+                cs = [chip[tiles[odd][j][0][0]] for j in js]
+                runs.append((at, B * len(js), T.trib[0:32, span(cs[0], cs[-1]), :, lists, :]))
+            for j in js:
+                sorted_at[j] = B * len(sorted_at)
+                todo.remove(j)
+        V.wait_ge(S["ld_w0"], 16)
+        V.quantize_mx(T.wq[:, 0:128], T.ws_[:, 0:128], T.wb[:, 0:512]).then_inc(S["wq0"], 1)
         V.wait_ge(S["ld_tri"], 32)
-        runs = [(32 * f + 16 * k, 16, T.trib[0:32, 4 * k:4 * k + 4, k if f else 1 - k, :]) for f in range(2) for k in range(2)]
-        runs.append((64, 16, T.trib[0:32, 2 * me:2 * me + 2, :, :]))
-        for j, (to, k, lists) in enumerate(runs):
-            if j == 3:
-                V.wait_ge(S["ld_w0"], 16)
-                V.quantize_mx(T.wq[:, 0:128], T.ws_[:, 0:128], T.wb[:, 0:512]).then_inc(S["wq0"], 1)
-            V.tensor_scalar(T.off1[0:32, to:to + k], lists, 4.0, 0.0, A.mult, A.max).then_inc(S["off0r"], 1)
+        for to, w, lists in runs:
+            V.tensor_scalar(T.off1[0:32, to // 16:(to + w) // 16], lists, 4.0, 0.0, A.mult, A.max).then_inc(S["off0r"], 1)
         V.wait_ge(S["off0r"], len(runs))
         for k in range(1, 4):
             V.tensor_copy(T.off1[32 * k:32 * k + 32, :], T.off1[0:32, :]).then_inc(S["off1r"], 1)
         for q in (V, C):
             q.wait_ge(S["off1r"], 3)
             q.wait_ge(S["ld_x"], 16)
-
-        def gather(p, c0, w, scalar, lists=None, dst="x", at=None):
-            lists = c0 if lists is None else lists
-            off = T.off1[:, lists // 16:(lists + w) // 16]
-            for t in range(4):
-                o = T.xg[:, 4 * c0 + t:4 * (c0 + w):4]
-                i = T.xb[:, t:4 * TOK].indirect(off)
-                (C.activation(o, i, F.Copy) if t < scalar else V.tensor_copy(o, i)).then_inc(S["gx%d" % p], 1)
-            V.wait_ge(S["gx%d" % p], 4)
-            at = c0 if at is None else at
-            V.quantize_mx(T[dst + "q"][:, at:at + w], T[dst + "s_"][:, at:at + w],
-                          T.xg[:, 4 * c0:4 * (c0 + w)]).then_inc(S["q1_%d" % p], 1)
-            g.wait_ge(S["q1_%d" % p], 1)
-
-        for f in range(2):
-            c0 = HA * f + B * partner
-            gather(3 * f, c0, B, 2)
-            send([move(mine, near if f else far + near, "x", c0, "r", B * f, B, True, "viaq%d" % f)])
-            send([move(mine, near, "x", c0, "r", B * f, B, False, "vias%d" % f)])
-            if f:
-                send([move(mine, near, "w", 256, "u", 256, 256, True, "inw")])
-                gather(4, HA + B * rest[0], PC, 2)
-                send(direct(f, rest, True))
-            else:
-                gather(1, B * longer[0], B, 2)
-                send(direct(f, longer[:1], True))
-                V.wait_ge(S["ld_w"], 16)
-                V.quantize_mx(T.wq[:, 128:512], T.ws_[:, 128:512], T.wb[:, 512:2048]).then_inc(S["wqr"], 1)
-                g.wait_ge(S["wqr"], 1)
-                send([move(mine, eng, "w", 128 * i, "u", 128 * i, 128 if i else 512, i > 0, "inw")
-                      for i, eng in share(range(2), near)])
-                gather(2, B * longer[1], B, 4)
-                send(direct(f, longer[1:], True))
-            send(direct(f, rest, False))
-        gather(5, B * me, B, 3, ALL + B * (sib % 2))
-        for code in (True, False):
-            send([move(worker(rank, sib), near, "x", B * me, "a", HB * OWN, B, code, "in1_4")])
-        gather(6, HA + B * me, B, 2, ALL + B * (rank % 2), "a", HB * OWN)
         E.wait_ge(S["wq0"], 1)
         E.wait_ge(S["wqr"], 1)
         wq, ws = T.wq, T.ws_
 
-    par = (rank + helps) % 2
+    def gather(js, scalar):
+        c0, w = min(sorted_at[j] for j in js), B * len(js)
+        for t in range(4):
+            o = T.xg[:, 4 * c0 + t:4 * (c0 + w):4]
+            i = T.xb[:, t:4 * TOK].indirect(T.off1[:, c0 // 16:(c0 + w) // 16])
+            (C.activation(o, i, F.Copy) if t < scalar else V.tensor_copy(o, i)).then_inc(S["gx%d" % js[0]], 1)
+        V.wait_ge(S["gx%d" % js[0]], 4)
+        for j in js:
+            _, dst, at, _ = source(tiles[odd][j][0])
+            V.quantize_mx(T[dst + "q"][:, at:at + B], T[dst + "s_"][:, at:at + B],
+                          T.xg[:, 4 * sorted_at[j]:4 * (sorted_at[j] + B)]).then_inc(S["q1_%d" % j], 1)
 
-    def step2(f, ranks, engines, code):
-        out = []
-        for b, eng in share(ranks, engines):
-            blk = 2 * me + (par if b // 2 != me else 0)
-            at = B * blk + (HB * (rank % 2) if b // 2 != me or par != b % 2 else B)
-            out.append(move(T.cores[b], eng, "h", PC * f + HB * (b % 4), "b", at, HB, code, "in2_%d" % blk))
-        return out
+    count, wave = [], ([], [])
 
-    own = [(("in1_4", 2 * n) if helps else ("q1_6", 1), OWN, [(OWN + half[f], f, me)]) for f in range(2)]
-    pair = [(("in1_%d" % (2 * f), (3 - f) * n // 2), PAIR[f], [(PAIR[f] + c % 2, f, c) for c in rest]) for f in range(2)]
-    via = [(("in1_%d" % (2 * f + 1), (1 + f) * n // 2), VIA[f] - 1, [(VIA[f], f, partner)]) for f in range(2)]
-    work = ([pair[0], own[0], via[0], own[1]] if helps else [own[0], own[1], pair[0], via[0]]) + [via[1], pair[1]]
-    for m, ((sem, count), lo, sources) in enumerate(work):
-        E.wait_ge(S[sem], count)
+    def product(w):
+        m = len(count)
+        at = [place[p] for p in w]
+        lo = min(at) if len(w) > 1 else place["tile" + w[0]] if "tile" + w[0] in place else at[0] - 1
+        wd = max(B, HB * len(w))
+        for p in w:
+            if p[0] == "X" and kind == "R":
+                wait(E, "q1_%d" % source(p + "r")[0], 1)
+            else:
+                wait(E, "in1_" + p, arrivals(p + kind.lower()))
         if m >= 2:
-            E.wait_ge(S["rl%d" % (m - 2)], 4 * len(work[m - 2][2]))
+            E.wait_ge(S["rl%d" % (m - 2)], count[m - 2])
         base = 2048 * (m % 2)
         for i in (0, 2, 1, 3):
-            E.matmul_mx(T.ps[:, base + 512 * i:base + 512 * i + B], wq[:, 128 * i:128 * i + 128],
-                        ws[:, 128 * i:128 * i + 128], T.aq[:, HB * lo:HB * lo + B], T.as_[:, HB * lo:HB * lo + B],
+            E.matmul_mx(T.ps[:, base + 512 * i:base + 512 * i + wd], wq[:, 128 * i:128 * i + 128],
+                        ws[:, 128 * i:128 * i + 128], T.aq[:, HB * lo:HB * lo + wd], T.as_[:, HB * lo:HB * lo + wd],
                         True, True).then_inc(S["m%d_%d" % (i, m)], 1)
+        by = OPT["evac"][kind][m]
         for i in range(4):
-            (C if i < 2 else V).wait_ge(S["m%d_%d" % (i, m)], 1)
-            for place, f, k in sources:
-                o = T.h[:, 4 * PC * f + 4 * k + i:4 * PC * (f + 1):16]
-                z = T.ps[:, base + 512 * i + HB * (place - lo):base + 512 * i + HB * (place - lo + 1)]
-                if i < 2:
+            (C if i < by else V).wait_ge(S["m%d_%d" % (i, m)], 1)
+            for p, j in zip(w, at):
+                f = int(p[1])
+                o = T.h[:, 4 * PC * f + 4 * chip[p[0]] + i:4 * PC * (f + 1):16]
+                z = T.ps[:, base + 512 * i + HB * (j - lo):base + 512 * i + HB * (j - lo + 1)]
+                if i < by:
                     C.activation(o, z, F.Relu, scale=0.043).then_inc(S["rl%d" % m], 1)
                 else:
                     V.tensor_scalar(o, z, 0.0, 0.043, A.max, A.mult).then_inc(S["rl%d" % m], 1)
-        if work[m] not in (via[0], pair[1]):
-            continue
-        for u in range(m + 1):
-            if work[u][2][0][1] == f:
-                V.wait_ge(S["rl%d" % u], 4 * len(work[u][2]))
-        for c in ([partner, me] if f else longer):
-            c0 = PC * f + B * (c % 2)
-            V.quantize_mx(T.hq[:, c0:c0 + B], T.hs_[:, c0:c0 + B], T.h[:, 4 * c0:4 * (c0 + B)]).then_inc(S["q2_%d" % c], 1)
-            if c != me:
-                g.wait_ge(S["q2_%d" % c], 1)
-                send(step2(f, groups[c], far, True))
-        send(step2(f, groups[partner] if f else groups[rest[0]] + groups[rest[1]], far, False))
-    g.wait_ge(S["q2_%d" % me], 1)
-    for code in (True, False):
-        send(step2(1, groups[me], near, code) if helps else step2(1, [sib], near[:n // 2], code))
-    if helps:
+        count.append(4 * len(w))
+        for f in set(int(p[1]) for p in w):
+            wave[f].append(m)
+
+    def column(c):
+        return PC * (c in own) + B * halves[c in own].index(c)
+
+    done = 0
+    for p in script[kind][odd]:
+        t = p[0]
+        if t[0] == "*":
+            product(t[1:].split("+"))
+        elif t[0] == "!":
+            c0 = column(chip[t[1]])
+            for u in wave[chip[t[1]] in own]:
+                wait(V, "rl%d" % u, count[u])
+            V.quantize_mx(T.hq[:, c0:c0 + B], T.hs_[:, c0:c0 + B], T.h[:, 4 * c0:4 * (c0 + B)]).then_inc(S["q2_" + t[1]], 1)
+        elif t in "ab":
+            step2(p)
+        elif t in "qs":
+            step1(p)
+        elif t in "QP":
+            tile = source(p[1] + "r")[0]
+            wait(g, "q1_%d" % tile, 1)
+            send([move(aid, every if t + p[1] in OPT["both"] else near, "x", B * tile, "r", B * tile, B, t == "Q",
+                       ("onqr" if t == "Q" else "onsr") + p[1])])
+        elif t == "W":
+            V.wait_ge(S["ld_w"], 16)
+            V.quantize_mx(T.wq[:, 128:512], T.ws_[:, 128:512], T.wb[:, 512:2048]).then_inc(S["wqr"], 1)
+        elif t in "vw":
+            wait(g, "wqr", 1)
+            send(weights(2 + (t == "w")))
+        elif t != "G0":
+            js = [done, done + 1] if len(t) == 3 else [done]
+            gather(js, int(t[1]))
+            done += len(js)
+        if t == "W" and ["v"] not in script[kind][odd]:
+            wait(g, "wqr", 1)
+            send(weights(2))
+    if kind != "R":
         g.wait_ge(S["ls"], left[0])
         return
 
@@ -243,13 +398,17 @@ def rank_program(g, core, T, topo):
     for k in range(4):
         V.tensor_copy(T.off2[32 * k:32 * k + 32, :], t[3]).then_inc(S["off2r"], 1)
 
+    def brought(k, c, o):
+        return sum(n // (2 * len([d for d in p[1].split(",") if d != "X"]))
+                   for p in script[k][o] if p[0] in "ab" and c in p[1].split(","))
+
     E.wait_ge(S["vqr"], 1)
-    for m in (4, 5):
-        E.wait_ge(S["rl%d" % m], 4 * len(work[m][2]))
+    for u in range(len(count))[-2:]:
+        E.wait_ge(S["rl%d" % u], count[u])
     bank = [0]
     copied = [0]
 
-    def product(q, sc, lo, w, on, copies):
+    def second(q, sc, lo, w, on, copies):
         sem, b0 = S["fm%d" % bank[0]], 512 * bank[0]
         bank[0] += 1
         E.matmul_mx(T.ps[:, b0:b0 + w], T.vq[:], T.vs_[:], q[:, lo:lo + w], sc[:, lo:lo + w], True, True).then_inc(sem, 1)
@@ -259,16 +418,17 @@ def rank_program(g, core, T, topo):
             (V.tensor_copy(y, z) if on is V else C.activation(y, z, F.Copy)).then_inc(S["fc"], 1)
             copied[0] += 1
 
-    E.wait_ge(S["q2_%d" % me], 1)
-    product(T.hq, T.hs_, PC + B * (me % 2), B, C, [(HB * par, HB, HA * par + HB * rank)])
-    for c in longer + [me, partner]:
+    E.wait_ge(S["q2_X"], 1)
+    second(T.hq, T.hs_, column(me), B, C, [(HB * par, HB, HA * par + HB * rank)])
+    for cls in OPT["last"]:
+        c = chip[cls]
         if c == me:
             E.wait_ge(S["in2_%d" % (2 * c)], 3 * n)
-            product(T.bq, T.bs_, PC * c, B + HB, V, [(0, B, HA * (1 - par) + B * c), (B, HB, HA * par + HB * sib)])
+            second(T.bq, T.bs_, PC * c, B + HB, V, [(0, B, HA * (1 - par) + B * c), (B, HB, HA * par + HB * sib)])
             continue
         for f in range(2):
-            E.wait_ge(S["in2_%d" % (2 * c + f)], 2 * n if c == partner else 3 * n // 2)
-            product(T.bq, T.bs_, PC * c + B * f, B, (C, V)[f], [(0, B, HA * f + B * c)])
+            E.wait_ge(S["in2_%d" % (2 * c + f)], brought("R", cls, f) + brought("H", cls, 1 - f))
+            second(T.bq, T.bs_, PC * c + B * f, B, (C, V)[f], [(0, B, HA * f + B * c)])
     Q = TOK // 4
     for q in (C, V):
         q.wait_ge(S["off2r"], 4)
@@ -278,11 +438,10 @@ def rank_program(g, core, T, topo):
         return T.yt[:, Q * u:Q * (u + 1)], T.yv[:].indirect(T.off2[:, Q * u // 16:Q * (u + 1) // 16])
 
     for u in range(2):
-        C.activation(*part(u), F.Copy).then_inc(S["ya%d" % u], 1)
-        V.tensor_copy(*part(2 + u)).then_inc(S["yb%d" % u], 1)
-    for q, sem, u, st in ((g.sync, "ya0", 0, "st1"), (g.sync, "yb0", 2, "st1"), (C, "ya1", 1, "st0"), (g.sync, "yb1", 3, "st1")):
-        q.wait_ge(S[sem], 1)
-        q.dma_start(T.y[:, Q * u:Q * (u + 1)], T.yt[:, Q * u:Q * (u + 1)]).then_inc(S[st], 16)
-    C.wait_ge(S["st0"], 16)
-    g.sync.wait_ge(S["st1"], 48)
+        C.activation(*part(2 * u), F.Copy).then_inc(S["yh%d" % u], 1)
+        V.tensor_copy(*part(2 * u + 1)).then_inc(S["yh%d" % u], 1)
+    for u in range(2):
+        g.sync.wait_ge(S["yh%d" % u], 2)
+        g.sync.dma_start(T.y[:, 2 * Q * u:2 * Q * (u + 1)], T.yt[:, 2 * Q * u:2 * Q * (u + 1)]).then_inc(S["st1"], 16)
+    g.sync.wait_ge(S["st1"], 32)
     g.wait_ge(S["ls"], left[0])

from concourse.bass import DstId, RemoteDMATransfer
from concourse.mybir import AluOpType, ActivationFunctionType, dt

OUT = ("!D a:D !Y a:Y b:D,Y", "!D !Y b:D,Y a:D a:Y")
END = " !S a:S b:S !X a:X b:X"
OPT = dict(
    R=("G2:S0r,Y0r s:S0r,Y0r q:S0r,Y0r G2:S0h,Y0h q:S0h,Y0h s:S0h,Y0h W G3:D0r,D0h q:D0r,D0h s:D0r,D0h "
       "G2J:D1r,D1h G0:Y1r,Y1h Q:D1 P:D1 q:Y1r,Y1h G3:X0r,X0h q:X0h s:Y1r,Y1h,X0h G3:S1r,S1h q:S1r,S1h s:S1r,S1h "
       "G3:X1r,X1h q:X1h s:X1h *X0+Y0 *D0+S0 !D a:D b:D !Y a:Y b:Y *X1+Y1 *D1+S1" + END,) * 2,
    H=("s:S0r q:S0r,S0h s:S0h q:D1r,D1h s:D1r,D1h *Y0+D0 *X0+S0 !D a:D b:D !Y a:Y b:Y *Y1+X1 *D1+S1" + END,) * 2,
    last="DYXS",
    weng="nfnn",
    halves="plane",
    both=(),
    flip=("qS1", "QD1", "qD1", "aS", "aY", "aD"),
    wat=0,
    one=1,
    evac=dict(R=[2, 2, 3, 2], H=[2, 2, 3, 2]),
    cut=(1, 2),
    hsplit=(),
)
N, TOK, TR = 8, 512, 16
B = N * TR
ALL = N * B
HB = B // 2
HA = ALL // 2
PC = 2 * B
CODES, PLANE = "float8_e4m3fn_x4", "uint8"

SCRATCH = {
    "trib": ("sbuf", [128, N // 2, 2, N // 2, 2], "int32"),
    "off1": ("sbuf", [128, ALL // 16], "uint16"),
    "pltb": ("sbuf", [128, TOK // 16], "int32"),
    "off2": ("sbuf", [128, TOK // 16], "uint16"),
    "xb": ("sbuf", [128, 4 * TOK], "bfloat16"),
    "wb": ("sbuf", [128, 2048], "bfloat16"),
    "vb": ("sbuf", [128, 512], "bfloat16"),
    "xg": ("sbuf", [128, 4 * ALL], "bfloat16"),
    "h": ("sbuf", [128, 4 * HA], "bfloat16"),
    "yv": ("sbuf", [128, ALL], "float32"),
    "yt": ("sbuf", [128, TOK], "float32"),
    "ps": ("psum", [128, 4096], "float32"),
}
for _name, _cols in (("w", 512), ("v", 128), ("x", ALL), ("h", HA), ("u", 512), ("r", ALL), ("a", 10 * HB), ("b", ALL)):
    SCRATCH[_name + "q"] = ("sbuf", [128, _cols], CODES)
    SCRATCH[_name + "s_"] = ("sbuf", [128, _cols], PLANE)
for _f in range(4):
    SCRATCH["n%d" % _f] = ("sbuf", [128, TOK // 16], "int32")
SEMAPHORES = (["ld_tri", "ld_x", "ld_w", "ld_w0", "wq0", "ld_v", "ld_plt", "off0r", "off1r", "off2r", "wqr", "vqr", "pt",
               "ls", "fc", "yh0", "yh1", "st1", "inw"]
              + [s + p + f for p in "DYS" for f in "01" for s in ("onqr", "onqh", "onsr", "onsh")]
              + ["in1_" + p + f for p in "DYSX" for f in "01"] + ["q2_" + p for p in "DYSX"]
              + [s + "%d" % p for p in range(8) for s in ("gx", "q1_", "rl", "m0_", "m1_", "m2_", "m3_", "in2_", "fm")])


def bits(engines):
    return sum(1 << e for e in engines)


def rank_program(g, core, T, topo):
    chips = []
    for c in T.cores:
        if topo.chip(c) not in chips:
            chips.append(topo.chip(c))
    groups = [[r for r in range(N) if topo.chip(T.cores[r]) == c] for c in chips]
    G = len(groups)

    def plane(m):
        return [c for c in range(G) if c == m or topo.same_plane(chips[m], chips[c])]

    def helper(r):
        c = T.cores[r]
        return [o for o in topo.cores_of(c) if T.rank_of(o) is None and all(topo.may_write(o, d) for d in T.cores)][r % 2]

    rank, kind = T.rank_of(core), "R"
    if rank is None:
        served = [r for r in range(N) if helper(r) == core]
        if not served:
            return
        rank, kind = served[0], "H"
    me, odd = rank // 2, rank % 2
    sib = [r for r in groups[me] if r != rank][0]
    other = [c for c in range(G) if c not in plane(me)]
    k = plane(me).index(me)
    chip = dict(D=other[k], Y=other[1 - k], S=plane(me)[1 - k], X=me)
    own = plane(me) if OPT["halves"] == "plane" else sorted([me, chip["D"]])
    halves = ([c for c in range(G) if c not in own], own)
    S = T.sem
    A = AluOpType
    F = ActivationFunctionType
    V, E, C = g.vector, g.tensor, g.scalar
    aid = helper(rank)
    every = topo.engines(core, T.cores[sib])
    far = topo.engines(core, T.cores[groups[chip["D"]][0]])
    near = [e for e in every if e not in far]
    n = len(far)
    script = {k: [[p.split(":") for p in s.split()] for s in OPT[k]] for k in "RH"}
    for k in "RH":
        l = script[k][1]
        for j in range(len(l) - 1):
            if l[j][1:] == l[j + 1][1:] and l[j][0] + l[j + 1][0] in ("qs", "ab", "QP") and l[j][0] + l[j][1][:2] in OPT["flip"]:
                l[j], l[j + 1] = l[j + 1], l[j]
    handed = [set(u for p in s if p[0] in "qs" for u in p[1].split(",")) for s in script["H"]]

    def target(u):
        return groups[chip[u[0]]][(rank + (u[2] == "h")) % 2]

    def half_of(c, f):
        return halves[f] if c in own else halves[1 - f]

    def key(u):
        return (chip[u[0]], target(u) % 2, half_of(chip[u[0]], int(u[1]))[0])

    tiles = [[sorted(p[1].split(","), key=key) for p in s if p[0][0] == "G"] for s in script["R"]]

    def calls(k, o):
        out = []
        for p in script[k][o]:
            if p[0] in ("q", "s"):
                us = p[1].split(",")
                off = [u for u in us if k == "H" or (u not in handed[o] and u[0] != "X")]
                on = [u for u in us if u not in off]
                lo, m = OPT["hsplit"][len(out)] if k == "H" and len(out) < len(OPT["hsplit"]) else (0, n)
                out.append((p, [(u, l is off, lo + j * (m // len(l)), m // len(l)) for l in (off, on) for j, u in enumerate(l)]))
        return out

    def arrivals(u):
        o = (odd + (u[2] == "h")) % 2
        return sum(w for k in "RH" for _, l in calls(k, o) for v, off, _, w in l if v == u and (k == "H" or u not in handed[o]))

    def landed(u, code):
        for p in script["R"][odd]:
            if p[0] == "QP"[not code] and p[1] == u[:2]:
                return "r", (2 * n if p[0] + p[1] in OPT["both"] else n)
        return u[2], [w for p, l in calls("R", odd) for v, _, _, w in l if v == u and p[0] == "qs"[not code]][0]

    def layout(k, o):
        at, out = 0, {}
        for p in script[k][o]:
            if p[0][0] != "*":
                continue
            w = p[0][1:].split("+")
            if k == "R" and w[0][0] == "X" and len(w) > 1 and w[1][0] != "X":
                out[w[0]], out["tile" + w[0]] = at + (len(w) - 1 if o == 0 else 1), at + (len(w) - 1 if o == 0 else 0)
                for j, s in enumerate(w[1:]):
                    out[s] = at + j + 2 * o
                at += len(w) + 1
            for s in w:
                if s in out:
                    continue
                if s[0] != "X" or k == "H":
                    out[s] = at
                    at += 1
                    continue
                for j, u in enumerate([t for t in tiles[o] if s + "r" in t][0]):
                    if u[0] == "X" and u[2] == "r":
                        out[u[:2]] = at + j
                        out["tile" + u[:2]] = at
                at += 2
        return out

    left = [0]

    def move(to, engines, src, lo, dst, at, w, code, sem):
        rid, pid, _ = topo.addr(to)
        a, b = T[src + ("q" if code else "s_")][:, lo:lo + w], T[dst + ("q" if code else "s_")][:, at:at + w]
        if code:
            a, b = a.bitcast(dt.uint8), b.bitcast(dt.uint8)
        left[0] += len(engines)
        return RemoteDMATransfer(dst_ids=[DstId(rid=rid, pnc=pid)], dma_engine_mask=bits(engines),
                                 remote_sem=S[sem], src=a, dst=b)

    def send(moves):
        g.remote_dma_fused(moves, local_sem=S["ls"])

    def share(items, engines):
        k = len(engines) // len(items)
        return [(it, engines[k * i:k * (i + 1)]) for i, it in enumerate(items)]

    place = layout(kind, odd)
    par = (rank + (kind == "H")) % 2

    def source(u):
        j = [j for j, t in enumerate(tiles[odd]) if u in t][0]
        t = tiles[odd][j]
        mine = [v for v in t if v[0] == "X" and v[2] == "r"]
        at = B * j + HB * t.index(u)
        if mine:
            return j, "a", HB * (layout("R", odd)["tile" + mine[0][:2]] + t.index(u)), at
        return j, "x", at, at

    waited = []

    def wait(q, sem, count):
        if (q is g, q is V, sem) not in waited:
            waited.append((q is g, q is V, sem))
            q.wait_ge(S[sem], count)

    def step1(p):
        code = p[0] == "q"
        out = []
        for u, off, j, w in [l for q, l in calls(kind, odd) if q is p][0]:
            tile, src, lo, at = source(u)
            eng = (far if off else near)[j:j + w]
            if kind == "H":
                k, count = landed(u, code)
                wait(g, ("onq" if code else "ons") + k + u[:2], count)
                src, lo = "r", at
            else:
                wait(g, "q1_%d" % tile, 1)
            if kind == "R" and u in handed[odd]:
                out.append(move(aid, eng, src, lo, "r", at, HB, code, ("onq" if code else "ons") + u[2] + u[:2]))
            else:
                a = target(u)
                out.append(move(T.cores[a] if u[2] == "r" else helper(a), eng, src, lo, "a",
                                HB * layout(u[2].upper(), a % 2)[u[:2]], HB, code, "in1_" + u[:2]))
        send(out)

    def step2(p):
        code = p[0] == "a"
        cs = p[1].split(",")
        out = []
        for on in (False, True):
            to = [b for c in cs for b in groups[chip[c]] if (c == "X") == on and T.cores[b] != core]
            if not to:
                continue
            for b, eng in share(to, (near[:n // 2 * len(to)] if on else far)):
                c = b // 2
                blk = 2 * me + (par if c != me else 0)
                at = B * blk + (HB * odd if c != me or par != b % 2 else B)
                out.append(move(T.cores[b], eng, "h", column(c) + HB * (b % 2), "b", at, HB, code, "in2_%d" % blk))
        for c in cs:
            wait(g, "q2_" + c, 1)
        send(out)

    def weights(j):
        eng = near if OPT["weng"][j] == "n" else far
        if j < 2:
            return [move(aid, eng[:n // OPT["cut"][j]], "w", 64 * j, "u", 64 * j, 64, True, "inw")]
        if j == 3:
            return [move(aid, eng, "w", 256, "u", 256, 256, True, "inw")]
        return [move(aid, e, "w", 128 * i, "u", 128 * i, 128 if i else 512, i > 0, "inw")
                for i, e in share(range(2 if ["w"] in script["R"][odd] else 4), eng)]

    sorted_at = {}
    if kind != "R":
        E.wait_ge(S["inw"], (1 + (["w"] in script["R"][odd])) * n + (n // OPT["cut"][0] + n // OPT["cut"][1] if OPT["one"] != 2 else n))
        wq, ws = T.uq, T.us_
    else:
        C.dma_start(T.wb[:, 0:512], T.w[:, 0:512]).then_inc(S["ld_w0"], 16)
        for k in range(2):
            g.sync.dma_start(T.trib[16 * k:16 * k + 16], T.tri[:]).then_inc(S["ld_tri"], 16)
        g.sync.dma_start(T.xb[:], T.x[:]).then_inc(S["ld_x"], 16)
        g.sync.dma_start(T.wb[:, 512:2048], T.w[:, 512:2048]).then_inc(S["ld_w"], 16)
        g.sync.dma_start(T.vb[:], T.vv[:]).then_inc(S["ld_v"], 16)
        for k in range(2):
            g.sync.dma_start(T.pltb[16 * k:16 * k + 16, :], T.plt[:]).then_inc(S["ld_plt"], 16)

        g.wait_ge(S["wq0"], 1)
        if OPT["one"] == 3:
            send(weights(1))
            send(weights(0))
        else:
            send(weights(0) + weights(1) if OPT["one"] == 1 else [move(aid, near, "w", 0, "u", 0, 128, True, "inw")])

        def span(a, b):
            return slice(a, b + 1, max(b - a, 1))

        runs, todo = [], list(range(len(tiles[odd])))
        while todo:
            u, v = tiles[odd][todo[0]]
            lists = span(*half_of(chip[u[0]], int(u[1])))
            at = B * len(sorted_at)
            if u[:2] != v[:2]:
                runs += [(at + HB * k, HB, T.trib[0:32, chip[w[0]], target(w) % 2, span(*half_of(chip[w[0]], int(w[1]))), :])
                         for k, w in enumerate((u, v))]
                js = todo[:1]
            else:
                js = [j for j in todo if tiles[odd][j][0][:2] == tiles[odd][j][1][:2] and tiles[odd][j][0][1] == u[1]
                      and (chip[tiles[odd][j][0][0]] in own) == (chip[u[0]] in own)]
                js.sort(key=lambda j: chip[tiles[odd][j][0][0]])
                cs = [chip[tiles[odd][j][0][0]] for j in js]
                runs.append((at, B * len(js), T.trib[0:32, span(cs[0], cs[-1]), :, lists, :]))
            for j in js:
                sorted_at[j] = B * len(sorted_at)
                todo.remove(j)
        V.wait_ge(S["ld_w0"], 16)
        V.quantize_mx(T.wq[:, 0:128], T.ws_[:, 0:128], T.wb[:, 0:512]).then_inc(S["wq0"], 1)
        V.wait_ge(S["ld_tri"], 32)
        for to, w, lists in runs:
            V.tensor_scalar(T.off1[0:32, to // 16:(to + w) // 16], lists, 4.0, 0.0, A.mult, A.max).then_inc(S["off0r"], 1)
        V.wait_ge(S["off0r"], len(runs))
        for k in range(1, 4):
            V.tensor_copy(T.off1[32 * k:32 * k + 32, :], T.off1[0:32, :]).then_inc(S["off1r"], 1)
        for q in (V, C):
            q.wait_ge(S["off1r"], 3)
            q.wait_ge(S["ld_x"], 16)
        E.wait_ge(S["wq0"], 1)
        E.wait_ge(S["wqr"], 1)
        wq, ws = T.wq, T.ws_

    def gather(js, scalar):
        c0, w = min(sorted_at[j] for j in js), B * len(js)
        for t in range(4):
            o = T.xg[:, 4 * c0 + t:4 * (c0 + w):4]
            i = T.xb[:, t:4 * TOK].indirect(T.off1[:, c0 // 16:(c0 + w) // 16])
            (C.activation(o, i, F.Copy) if t < scalar else V.tensor_copy(o, i)).then_inc(S["gx%d" % js[0]], 1)
        V.wait_ge(S["gx%d" % js[0]], 4)
        for j in js:
            _, dst, at, _ = source(tiles[odd][j][0])
            V.quantize_mx(T[dst + "q"][:, at:at + B], T[dst + "s_"][:, at:at + B],
                          T.xg[:, 4 * sorted_at[j]:4 * (sorted_at[j] + B)]).then_inc(S["q1_%d" % j], 1)

    count, wave = [], ([], [])

    def product(w):
        m = len(count)
        at = [place[p] for p in w]
        lo = min(at) if len(w) > 1 else place["tile" + w[0]] if "tile" + w[0] in place else at[0] - 1
        wd = max(B, HB * len(w))
        for p in w:
            if p[0] == "X" and kind == "R":
                wait(E, "q1_%d" % source(p + "r")[0], 1)
            else:
                wait(E, "in1_" + p, arrivals(p + kind.lower()))
        if m >= 2:
            E.wait_ge(S["rl%d" % (m - 2)], count[m - 2])
        base = 2048 * (m % 2)
        for i in (0, 2, 1, 3):
            E.matmul_mx(T.ps[:, base + 512 * i:base + 512 * i + wd], wq[:, 128 * i:128 * i + 128],
                        ws[:, 128 * i:128 * i + 128], T.aq[:, HB * lo:HB * lo + wd], T.as_[:, HB * lo:HB * lo + wd],
                        True, True).then_inc(S["m%d_%d" % (i, m)], 1)
        by = OPT["evac"][kind][m]
        for i in range(4):
            (C if i < by else V).wait_ge(S["m%d_%d" % (i, m)], 1)
            for p, j in zip(w, at):
                f = int(p[1])
                o = T.h[:, 4 * PC * f + 4 * chip[p[0]] + i:4 * PC * (f + 1):16]
                z = T.ps[:, base + 512 * i + HB * (j - lo):base + 512 * i + HB * (j - lo + 1)]
                if i < by:
                    C.activation(o, z, F.Relu, scale=0.043).then_inc(S["rl%d" % m], 1)
                else:
                    V.tensor_scalar(o, z, 0.0, 0.043, A.max, A.mult).then_inc(S["rl%d" % m], 1)
        count.append(4 * len(w))
        for f in set(int(p[1]) for p in w):
            wave[f].append(m)

    def column(c):
        return PC * (c in own) + B * halves[c in own].index(c)

    done = 0
    for p in script[kind][odd]:
        t = p[0]
        if t[0] == "*":
            product(t[1:].split("+"))
        elif t[0] == "!":
            c0 = column(chip[t[1]])
            for u in wave[chip[t[1]] in own]:
                wait(V, "rl%d" % u, count[u])
            V.quantize_mx(T.hq[:, c0:c0 + B], T.hs_[:, c0:c0 + B], T.h[:, 4 * c0:4 * (c0 + B)]).then_inc(S["q2_" + t[1]], 1)
        elif t in "ab":
            step2(p)
        elif t in "qs":
            step1(p)
        elif t in "QP":
            tile = source(p[1] + "r")[0]
            wait(g, "q1_%d" % tile, 1)
            send([move(aid, every if t + p[1] in OPT["both"] else near, "x", B * tile, "r", B * tile, B, t == "Q",
                       ("onqr" if t == "Q" else "onsr") + p[1])])
        elif t == "W":
            V.wait_ge(S["ld_w"], 16)
            V.quantize_mx(T.wq[:, 128:512], T.ws_[:, 128:512], T.wb[:, 512:2048]).then_inc(S["wqr"], 1)
        elif t in "vw":
            wait(g, "wqr", 1)
            send(weights(2 + (t == "w")))
        elif t != "G0":
            js = [done, done + 1] if len(t) == 3 else [done]
            gather(js, int(t[1]))
            done += len(js)
        if t == "W" and ["v"] not in script[kind][odd]:
            wait(g, "wqr", 1)
            send(weights(2))
    if kind != "R":
        g.wait_ge(S["ls"], left[0])
        return

    V.wait_ge(S["ld_v"], 16)
    V.quantize_mx(T.vq[:], T.vs_[:], T.vb[:]).then_inc(S["vqr"], 1)
    t = [T["n%d" % i][0:32, :] for i in range(4)]
    V.wait_ge(S["ld_plt"], 32)
    V.tensor_scalar(t[0], T.pltb[0:32, :], 255, None, A.bitwise_and).then_inc(S["pt"], 1)
    V.tensor_scalar(t[1], T.pltb[0:32, :], 8, None, A.logical_shift_right).then_inc(S["pt"], 1)
    V.wait_ge(S["pt"], 2)
    V.tensor_scalar(t[2], t[0], 4.0, None, A.mult).then_inc(S["pt"], 1)
    V.wait_ge(S["pt"], 3)
    V.tensor_tensor(t[3], t[2], t[1], A.add).then_inc(S["pt"], 1)
    V.wait_ge(S["pt"], 4)
    for k in range(4):
        V.tensor_copy(T.off2[32 * k:32 * k + 32, :], t[3]).then_inc(S["off2r"], 1)

    def brought(k, c, o):
        return sum(n // (2 * len([d for d in p[1].split(",") if d != "X"]))
                   for p in script[k][o] if p[0] in "ab" and c in p[1].split(","))

    E.wait_ge(S["vqr"], 1)
    for u in range(len(count))[-2:]:
        E.wait_ge(S["rl%d" % u], count[u])
    bank = [0]
    copied = [0]

    def second(q, sc, lo, w, on, copies):
        sem, b0 = S["fm%d" % bank[0]], 512 * bank[0]
        bank[0] += 1
        E.matmul_mx(T.ps[:, b0:b0 + w], T.vq[:], T.vs_[:], q[:, lo:lo + w], sc[:, lo:lo + w], True, True).then_inc(sem, 1)
        on.wait_ge(sem, 1)
        for a, b, to in copies:
            z, y = T.ps[:, b0 + a:b0 + a + b], T.yv[:, to:to + b]
            (V.tensor_copy(y, z) if on is V else C.activation(y, z, F.Copy)).then_inc(S["fc"], 1)
            copied[0] += 1

    E.wait_ge(S["q2_X"], 1)
    second(T.hq, T.hs_, column(me), B, C, [(HB * par, HB, HA * par + HB * rank)])
    for cls in OPT["last"]:
        c = chip[cls]
        if c == me:
            E.wait_ge(S["in2_%d" % (2 * c)], 3 * n)
            second(T.bq, T.bs_, PC * c, B + HB, V, [(0, B, HA * (1 - par) + B * c), (B, HB, HA * par + HB * sib)])
            continue
        for f in range(2):
            E.wait_ge(S["in2_%d" % (2 * c + f)], brought("R", cls, f) + brought("H", cls, 1 - f))
            second(T.bq, T.bs_, PC * c + B * f, B, (C, V)[f], [(0, B, HA * f + B * c)])
    Q = TOK // 4
    for q in (C, V):
        q.wait_ge(S["off2r"], 4)
        q.wait_ge(S["fc"], copied[0])

    def part(u):
        return T.yt[:, Q * u:Q * (u + 1)], T.yv[:].indirect(T.off2[:, Q * u // 16:Q * (u + 1) // 16])

    for u in range(2):
        C.activation(*part(2 * u), F.Copy).then_inc(S["yh%d" % u], 1)
        V.tensor_copy(*part(2 * u + 1)).then_inc(S["yh%d" % u], 1)
    for u in range(2):
        g.sync.wait_ge(S["yh%d" % u], 2)
        g.sync.dma_start(T.y[:, 2 * Q * u:2 * Q * (u + 1)], T.yt[:, 2 * Q * u:2 * Q * (u + 1)]).then_inc(S["st1"], 16)
    g.sync.wait_ge(S["st1"], 32)
    g.wait_ge(S["ls"], left[0])
